import numpy as np
import ml_dtypes


def mxq(x, axis, fmt="e4m3"):
    dtype, down = {"e4m3": (ml_dtypes.float8_e4m3fn, 7), "e5m2": (ml_dtypes.float8_e5m2, 14)}[fmt]
    v = np.moveaxis(np.asarray(x, np.float32).astype(ml_dtypes.bfloat16).astype(np.float64), axis, -1)
    blocks = v.reshape(v.shape[:-1] + (-1, 32))
    amax = np.abs(blocks).max(-1, keepdims=True)
    byte = np.maximum(np.where(amax > 0, np.frexp(amax)[1] - 1 + 127, 0) - down, 1)
    scale = np.exp2(byte - 127.0)
    codes = (blocks / scale).astype(np.float32).astype(dtype).astype(np.float64)
    return np.moveaxis((codes * scale).reshape(v.shape), -1, axis)


WIDE = False


def mx_kscale(k):
    if not WIDE:
        return np.ones(k)
    levels = np.array([10, -10, 5, -5, 0])
    if k % 512:
        return np.exp2(np.random.permutation(np.resize(levels, k // 32))).repeat(32)
    a = np.empty((k // 512, 16))
    for p in range(k // 512):
        a[p, :8] = np.random.permutation(np.resize(levels, 8))
        for g in range(8):
            far = levels[np.abs(levels - a[p, g]) >= 10]
            a[p, g + 8] = far[np.random.randint(len(far))]
    return np.exp2(a.ravel()).repeat(32)


def f64(x):
    return np.asarray(x).astype(np.float64)


def striped(idx):
    return np.tile(idx.reshape(-1, 16).T, (8, 1)).astype(np.uint16)


def unstriped(offs):
    return offs[:16].T.reshape(-1).astype(np.int64)


def pack_weight(w):
    k, n = w.shape
    w = f64(np.asarray(w, np.float32).astype(ml_dtypes.bfloat16)).reshape(k // 32, 32, n)
    amax = np.abs(w).max(1)
    byte = np.clip(np.where(amax > 0, np.frexp(amax)[1] - 1 + 127 - 7, 1), 1, 254)
    scaled = (w * np.exp2(127.0 - byte)[:, None, :]).reshape(k, n).astype(np.float32)
    words = np.ascontiguousarray(scaled.reshape(k // 512, 128, 4, n).transpose(0, 1, 3, 2)).astype(ml_dtypes.float8_e4m3fn).view(np.uint8)
    return words, np.ascontiguousarray(byte.astype(np.uint8).reshape(k // 512, 16, n))


def unpack_weight(words, scales):
    g, p, n, _ = words.shape
    vals = np.ascontiguousarray(words).view(ml_dtypes.float8_e4m3fn).astype(np.float64) * np.repeat(np.exp2(scales.astype(np.float64) - 127.0), 8, axis=1)[..., None]
    return vals.transpose(0, 1, 3, 2).reshape(g * 512, n)

def planes(y):
    n, m = y.shape
    v = y.astype(np.float32).astype(ml_dtypes.bfloat16).astype(np.float64).reshape(n // 32, 32, m)
    top = np.abs(v).max(1)
    byte = np.clip(np.where(top > 0, np.frexp(top)[1] - 1 + 127 - 7, 1), 1, 254)
    codes = (v * np.exp2(127.0 - byte)[:, None, :]).reshape(n, m).astype(np.float32).astype(ml_dtypes.float8_e4m3fn).view(np.uint8)
    words = codes.reshape(n // 512, 128, 4, m).transpose(0, 1, 3, 2)
    return np.ascontiguousarray(words), np.ascontiguousarray(byte.astype(np.uint8).reshape(n // 512, 16, m))


K, T, N, U = 512, 512, 512, 1024
P = 2 ** 7


def setup_inputs():
    n = np.random.standard_normal
    s = mx_kscale(K)[:, None]
    packed_xT = pack_weight(n((K, T)) * s)
    return {
        "x_words": packed_xT[0],
        "x_scales": packed_xT[1],
        "mem": n((N, U)).astype(np.float32),
        "w1": (n((K, N)) / np.sqrt(K) / s).astype(np.float32),
        "old": np.tile(np.random.uniform(0.5, 0.95, T), (P, 1)).astype(np.float32),
        "new": np.tile(np.random.uniform(0.05, 0.5, T), (P, 1)).astype(np.float32),
        "slot": striped(np.random.permutation(U)[:T]),
    }


def reference(x_words, x_scales, mem, w1, old, new, slot):
    xq = unpack_weight(x_words, x_scales)
    y = mxq(f64(w1), 0, "e4m3").T @ xq
    out = f64(mem).copy()
    out[:, unstriped(slot)] = f64(mem)[:, unstriped(slot)] * f64(old)[:1] + y * f64(new)[:1]
    return (out,) + planes(out)

@@ -1,0 +1,162 @@
+from contextlib import ExitStack
+
+import concourse.mybir as mybir
+from concourse.masks import make_identity
+
+K, T, N, U = 512, 512, 512, 1024
+P = 128
+PACK = 4
+BLOCKS = T // P
+CHUNKS = 4
+CHUNK = U // CHUNKS
+FLOPS = 2 * K * N * T
+
+F32 = mybir.dt.float32
+BF16 = mybir.dt.bfloat16
+I32 = mybir.dt.int32
+U32 = mybir.dt.uint32
+U16 = mybir.dt.uint16
+U8 = mybir.dt.uint8
+FP8X4 = mybir.dt.float8_e4m3fn_x4
+MULT = mybir.AluOpType.mult
+ADD = mybir.AluOpType.add
+COPY = mybir.ActivationFunctionType.Copy
+
+
+def tile_picked_wema_none_lo_kernel(
+    tc, x_words, x_scales, mem, w1, old, new, slot, out_0, out_1, out_2
+):
+    nc = tc.nc
+    mem_rows = mem.rearrange("(p t) u -> p t u", t=PACK)
+    out_rows = out_0.rearrange("(p t) u -> p t u", t=PACK)
+    w_rows = w1.rearrange("(p j) c -> p j c", j=PACK)
+
+    with ExitStack() as ctx:
+        keep = ctx.enter_context(tc.tile_pool(name="keep", bufs=1))
+        psum = ctx.enter_context(tc.psum_pool(name="psum", bufs=1))
+
+        offsets = keep.tile([P, T // 16], U16, name="offsets")
+        old_sb = keep.tile([P, T], F32, name="old_sb")
+        new_rows = keep.tile([P, P], F32, name="new_rows")
+        windows = [keep.tile([P, U], F32, name="window%d" % t) for t in range(PACK)]
+        w_raw = [keep.tile([P, PACK, N // 2], F32, name="w_raw%d" % h) for h in range(2)]
+        x_codes = keep.tile([P, T], I32, name="x_codes", align_bytes=64)
+        x_plane = keep.tile([P, T], U8, name="x_plane", align_bytes=64)
+        ident = keep.tile([P, P], F32, name="ident")
+
+        nc.gpsimd.memset(x_plane[:].bitcast(I32), 0)
+        nc.gpsimd.memset(new_rows[:], 0.0)
+        make_identity(nc, ident[:])
+
+        nc.sync.dma_start(offsets[:], slot)
+        nc.sync.dma_start(windows[0][:], mem_rows[:, 0, :])
+        nc.sync.dma_start(old_sb[:], old)
+        nc.sync.dma_start(new_rows[0:BLOCKS, :], new[0].rearrange("(b i) -> b i", b=BLOCKS))
+        for q in range(4):
+            nc.sync.dma_start(
+                x_plane[32 * q : 32 * q + 4, :].bitcast(I32), x_scales[0, 4 * q : 4 * q + 4, :].bitcast(I32)
+            )
+        for h in range(2):
+            nc.sync.dma_start(w_raw[h][:], w_rows[:, :, h * (N // 2) : (h + 1) * (N // 2)])
+        nc.sync.dma_start(x_codes[:], x_words[0].rearrange("p n t -> p (n t)").bitcast(I32))
+        for t in range(1, PACK):
+            nc.sync.dma_start(windows[t][:], mem_rows[:, t, :])
+
+        new_turned = psum.tile([P, P], F32, name="new_turned", tag="back3")
+        nc.tensor.transpose(new_turned[:], new_rows[:], ident[:])
+        new_col = keep.tile([P, BLOCKS], F32, name="new_col")
+        nc.scalar.activation(new_col[:], new_turned[:, 0:BLOCKS], COPY)
+
+        kept = [keep.tile([P, T], F32, name="kept%d" % t) for t in range(PACK)]
+        fresh = [keep.tile([P, T], F32, name="fresh%d" % t) for t in range(PACK)]
+
+        def gather(t):
+            nc.vector.tensor_tensor(kept[t][:], windows[t][:].indirect(offsets[:]), old_sb[:], MULT)
+
+        gather(0)
+
+        w_codes = keep.tile([P, N], U32, name="w_codes", align_bytes=64)
+        w_plane = keep.tile([P, N], U8, name="w_plane", align_bytes=64)
+        w_grouped = [keep.tile([P, N // 2, PACK], BF16, name="w_grouped%d" % h, align_bytes=64) for h in range(2)]
+        for h in range(2):
+            dst = w_grouped[h][:].rearrange("p (c i) j -> p c j i", i=4)
+            src = w_raw[h][:].rearrange("p j (c i) -> p c j i", i=4)
+            if h == 0:
+                nc.scalar.copy(out=dst, in_=src)
+            else:
+                nc.vector.tensor_copy(out=dst, in_=src)
+        for h in range(2):
+            cols = slice(h * (N // 2), (h + 1) * (N // 2))
+            nc.vector.quantize_mx(
+                out=w_codes[:, cols].bitcast(FP8X4),
+                scales=w_plane[:, cols],
+                in_=w_grouped[h][:].rearrange("p c j -> p (c j)"),
+            )
+
+        first = [keep.tile([P, P], F32, name="first%d" % b) for b in range(BLOCKS)]
+        rest = [keep.tile([P, PACK - 1, P], F32, name="rest%d" % b) for b in range(BLOCKS)]
+        accs = []
+        for b in range(BLOCKS):
+            acc = psum.tile([P, N], F32, name="acc%d" % b)
+            cols = slice(b * P, (b + 1) * P)
+            nc.tensor.matmul_mx(
+                out=acc[:],
+                lhsT=x_codes[:, cols].bitcast(FP8X4),
+                lhsT_scale=x_plane[:, cols],
+                rhs=w_codes[:].bitcast(FP8X4),
+                rhs_scale=w_plane[:],
+                start=True,
+                stop=True,
+            )
+            dealt = acc[:].rearrange("j (p t) -> j t p", t=PACK)
+            accs.append(dealt)
+            nc.scalar.activation(first[b][:], dealt[:, 0, :], COPY, scale=new_col[:, b : b + 1])
+
+        def turn_back(t):
+            back = psum.tile([P, T], F32, name="back", tag="back%d" % t)
+            for b in range(BLOCKS):
+                src = first[b][:] if t == 0 else rest[b][:, t - 1, :]
+                nc.tensor.transpose(back[:, b * P : (b + 1) * P], src, ident[:])
+            nc.scalar.copy(out=fresh[t][:], in_=back[:])
+
+        turn_back(0)
+        for b in range(BLOCKS):
+            nc.scalar.activation(rest[b][:], accs[b][:, 1:PACK, :], COPY, scale=new_col[:, b : b + 1])
+        for t in range(1, PACK):
+            turn_back(t)
+
+        grouped = [keep.tile([P, CHUNK, PACK], BF16, name="grouped%d" % c, align_bytes=64) for c in range(CHUNKS)]
+        gather(1)
+        gather(2)
+        for t in range(PACK):
+            if t == PACK - 1:
+                gather(t)
+            nc.vector.tensor_tensor(windows[t][:].indirect(offsets[:]), kept[t][:], fresh[t][:], ADD)
+            nc.sync.dma_start(out_rows[:, t, :], windows[t][:])
+            for c in range(CHUNKS):
+                src = windows[t][:, c * CHUNK : (c + 1) * CHUNK]
+                if t == 2 and c < 2:
+                    nc.scalar.copy(out=grouped[c][:, :, 2:4], in_=src.unsqueeze(2).to_broadcast([P, CHUNK, 2]))
+                elif t == 3 and c < 2:
+                    nc.vector.tensor_copy(out=grouped[c][:, :, t], in_=src)
+                else:
+                    nc.scalar.copy(out=grouped[c][:, :, t], in_=src)
+
+        y_plane = keep.tile([P, U], U8, name="y_plane", align_bytes=64)
+        y_codes = keep.tile([P, U], I32, name="y_codes", align_bytes=64)
+        words_out = out_1[0].rearrange("p n t -> p (n t)").bitcast(I32)
+        for c in range(CHUNKS):
+            cols = slice(c * CHUNK, (c + 1) * CHUNK)
+            nc.vector.quantize_mx(
+                out=y_codes[:, cols].bitcast(FP8X4),
+                scales=y_plane[:, cols],
+                in_=grouped[c][:].rearrange("p c t -> p (c t)"),
+            )
+            if c > 0:
+                stored = slice(0, 2 * CHUNK) if c == 1 else cols
+                nc.sync.dma_start(words_out[:, stored], y_codes[:, stored])
+        for q in range(4):
+            queue = nc.sync if q % 2 else nc.scalar
+            queue.dma_start(
+                out_2[0, 4 * q : 4 * q + 4, :].bitcast(I32), y_plane[32 * q : 32 * q + 4, :].bitcast(I32)
+            )

@@ -39,105 +39,133 @@ def tile_picked_wema_none_lo_kernel(
         old_sb = keep.tile([P, T], F32, name="old_sb")
         new_rows = keep.tile([P, P], F32, name="new_rows")
         windows = [keep.tile([P, U], F32, name="window%d" % t) for t in range(PACK)]
-        w_raw = [keep.tile([P, PACK, N // 2], F32, name="w_raw%d" % h) for h in range(2)]
+        w_raw = [keep.tile([P, 2, N], F32, name="w_raw%d" % h) for h in range(2)]
         x_codes = keep.tile([P, T], I32, name="x_codes", align_bytes=64)
         x_plane = keep.tile([P, T], U8, name="x_plane", align_bytes=64)
         ident = keep.tile([P, P], F32, name="ident")
 
-        nc.gpsimd.memset(x_plane[:].bitcast(I32), 0)
         nc.gpsimd.memset(new_rows[:], 0.0)
+        nc.gpsimd.memset(x_plane[:].bitcast(I32), 0)
         make_identity(nc, ident[:])
 
+        old_col = keep.tile([P, PACK], F32, name="old_col")
+        nc.sync.dma_start(w_raw[0][:], w_rows[:, 0:2, :])
+        nc.sync.dma_start(old_col[:], old[0].rearrange("(p i) -> p i", i=PACK))
         nc.sync.dma_start(offsets[:], slot)
-        nc.sync.dma_start(windows[0][:], mem_rows[:, 0, :])
-        nc.sync.dma_start(old_sb[:], old)
         nc.sync.dma_start(new_rows[0:BLOCKS, :], new[0].rearrange("(b i) -> b i", b=BLOCKS))
+        nc.sync.dma_start(w_raw[1][:], w_rows[:, 2:4, :])
+        nc.sync.dma_start(windows[0][:], mem_rows[:, 0, :])
+        nc.sync.dma_start(x_codes[:], x_words[0].rearrange("p n t -> p (n t)").bitcast(I32))
         for q in range(4):
             nc.sync.dma_start(
                 x_plane[32 * q : 32 * q + 4, :].bitcast(I32), x_scales[0, 4 * q : 4 * q + 4, :].bitcast(I32)
             )
-        for h in range(2):
-            nc.sync.dma_start(w_raw[h][:], w_rows[:, :, h * (N // 2) : (h + 1) * (N // 2)])
-        nc.sync.dma_start(x_codes[:], x_words[0].rearrange("p n t -> p (n t)").bitcast(I32))
         for t in range(1, PACK):
             nc.sync.dma_start(windows[t][:], mem_rows[:, t, :])
 
-        new_turned = psum.tile([P, P], F32, name="new_turned", tag="back3")
+        old_spread = psum.tile([P, PACK, P], F32, name="old_spread", tag="turn2")
+        for i in range(PACK):
+            nc.tensor.transpose(old_spread[:, i, :], old_col[:, i : i + 1].to_broadcast([P, P]), ident[:])
+        nc.scalar.activation(
+            old_sb[:].rearrange("q (p i) -> q p i", i=PACK), old_spread[:].rearrange("q i p -> q p i"), COPY
+        )
+
+        new_turned = psum.tile([P, P], F32, name="new_turned", tag="turn3")
         nc.tensor.transpose(new_turned[:], new_rows[:], ident[:])
         new_col = keep.tile([P, BLOCKS], F32, name="new_col")
         nc.scalar.activation(new_col[:], new_turned[:, 0:BLOCKS], COPY)
 
-        kept = [keep.tile([P, T], F32, name="kept%d" % t) for t in range(PACK)]
+        kept = []
         fresh = [keep.tile([P, T], F32, name="fresh%d" % t) for t in range(PACK)]
 
         def gather(t):
-            nc.vector.tensor_tensor(kept[t][:], windows[t][:].indirect(offsets[:]), old_sb[:], MULT)
-
-        gather(0)
+            looked_up = keep.tile([P, T], F32, name="looked_up", tag="kept%d" % (t % 3))
+            nc.vector.tensor_tensor(looked_up[:], windows[t][:].indirect(offsets[:]), old_sb[:], MULT)
+            kept.append(looked_up)
 
         w_codes = keep.tile([P, N], U32, name="w_codes", align_bytes=64)
         w_plane = keep.tile([P, N], U8, name="w_plane", align_bytes=64)
-        w_grouped = [keep.tile([P, N // 2, PACK], BF16, name="w_grouped%d" % h, align_bytes=64) for h in range(2)]
+        w_grouped = keep.tile([P, PACK, P, PACK], BF16, name="w_grouped", align_bytes=64)
         for h in range(2):
-            dst = w_grouped[h][:].rearrange("p (c i) j -> p c j i", i=4)
-            src = w_raw[h][:].rearrange("p j (c i) -> p c j i", i=4)
-            if h == 0:
-                nc.scalar.copy(out=dst, in_=src)
-            else:
-                nc.vector.tensor_copy(out=dst, in_=src)
-        for h in range(2):
-            cols = slice(h * (N // 2), (h + 1) * (N // 2))
+            nc.vector.tensor_copy(
+                out=w_grouped[:, :, :, 2 * h : 2 * h + 2].rearrange("p t m j -> p m t j"),
+                in_=w_raw[h][:].rearrange("p j (m t) -> p m t j", t=PACK),
+            )
+        stages = [slice(0, 1), slice(1, 3), slice(3, 4)]
+        for ts in stages:
+            cols = slice(ts.start * P, ts.stop * P)
             nc.vector.quantize_mx(
                 out=w_codes[:, cols].bitcast(FP8X4),
                 scales=w_plane[:, cols],
-                in_=w_grouped[h][:].rearrange("p c j -> p (c j)"),
+                in_=w_grouped[:, ts, :, :].rearrange("p t m j -> p (t m j)"),
             )
 
-        first = [keep.tile([P, P], F32, name="first%d" % b) for b in range(BLOCKS)]
-        rest = [keep.tile([P, PACK - 1, P], F32, name="rest%d" % b) for b in range(BLOCKS)]
-        accs = []
-        for b in range(BLOCKS):
-            acc = psum.tile([P, N], F32, name="acc%d" % b)
-            cols = slice(b * P, (b + 1) * P)
+        def project(acc, b, ts):
+            rows = slice(b * P, (b + 1) * P)
+            cols = slice(ts.start * P, ts.stop * P)
             nc.tensor.matmul_mx(
-                out=acc[:],
-                lhsT=x_codes[:, cols].bitcast(FP8X4),
-                lhsT_scale=x_plane[:, cols],
-                rhs=w_codes[:].bitcast(FP8X4),
-                rhs_scale=w_plane[:],
+                out=acc,
+                lhsT=x_codes[:, rows].bitcast(FP8X4),
+                lhsT_scale=x_plane[:, rows],
+                rhs=w_codes[:, cols].bitcast(FP8X4),
+                rhs_scale=w_plane[:, cols],
                 start=True,
                 stop=True,
             )
-            dealt = acc[:].rearrange("j (p t) -> j t p", t=PACK)
-            accs.append(dealt)
-            nc.scalar.activation(first[b][:], dealt[:, 0, :], COPY, scale=new_col[:, b : b + 1])
 
-        def turn_back(t):
-            back = psum.tile([P, T], F32, name="back", tag="back%d" % t)
+        first = []
+        for b in range(BLOCKS):
+            acc = psum.tile([P, P], F32, name="acc_first", tag="lead%d" % b)
+            project(acc[:], b, stages[0])
+            scaled = keep.tile([P, P], F32, name="first%d" % b)
+            nc.scalar.activation(scaled[:], acc[:], COPY, scale=new_col[:, b : b + 1])
+            first.append(scaled)
+        for b in range(BLOCKS):
+            piece = psum.tile([P, P], F32, name="piece", tag="turn%d" % b)
+            nc.tensor.transpose(piece[:], first[b][:], ident[:])
+            nc.scalar.copy(out=fresh[0][:, b * P : (b + 1) * P], in_=piece[:])
+
+        rest = []
+        for b in range(BLOCKS):
+            acc = psum.tile([P, PACK - 1, P], F32, name="acc_rest", tag="turn%d" % b)
+            project(acc[:, 0:2, :].rearrange("j t p -> j (t p)"), b, stages[1])
+            project(acc[:, 2, :], b, stages[2])
+            if b < BLOCKS - 1:
+                others = keep.tile([P, PACK - 1, P], F32, name="others%d" % b)
+                nc.scalar.activation(others[:], acc[:], COPY, scale=new_col[:, b : b + 1])
+                rest.append([others[:, i, :] for i in range(PACK - 1)])
+            else:
+                ones = []
+                for i in range(PACK - 1):
+                    one = keep.tile([P, P], F32, name="one", tag="stage%d" % i, align_bytes=64)
+                    nc.scalar.activation(one[:], acc[:, i, :], COPY, scale=new_col[:, b : b + 1])
+                    ones.append(one[:])
+                rest.append(ones)
+        for t in range(1, PACK):
+            back = psum.tile([P, T], F32, name="back", tag="lead%d" % t)
             for b in range(BLOCKS):
-                src = first[b][:] if t == 0 else rest[b][:, t - 1, :]
-                nc.tensor.transpose(back[:, b * P : (b + 1) * P], src, ident[:])
+                nc.tensor.transpose(back[:, b * P : (b + 1) * P], rest[b][t - 1], ident[:])
             nc.scalar.copy(out=fresh[t][:], in_=back[:])
 
-        turn_back(0)
-        for b in range(BLOCKS):
-            nc.scalar.activation(rest[b][:], accs[b][:, 1:PACK, :], COPY, scale=new_col[:, b : b + 1])
-        for t in range(1, PACK):
-            turn_back(t)
-
-        grouped = [keep.tile([P, CHUNK, PACK], BF16, name="grouped%d" % c, align_bytes=64) for c in range(CHUNKS)]
-        gather(1)
-        gather(2)
+        spans = [slice(0, 512), slice(512, 768), slice(768, 1024)]
+        grouped = [
+            keep.tile(
+                [P, spans[c].stop - spans[c].start, PACK], BF16, name="grouped", tag="stage%d" % c, align_bytes=64
+            )
+            for c in range(3)
+        ]
+        for t in range(PACK - 1):
+            gather(t)
         for t in range(PACK):
             if t == PACK - 1:
                 gather(t)
             nc.vector.tensor_tensor(windows[t][:].indirect(offsets[:]), kept[t][:], fresh[t][:], ADD)
             nc.sync.dma_start(out_rows[:, t, :], windows[t][:])
-            for c in range(CHUNKS):
-                src = windows[t][:, c * CHUNK : (c + 1) * CHUNK]
-                if t == 2 and c < 2:
-                    nc.scalar.copy(out=grouped[c][:, :, 2:4], in_=src.unsqueeze(2).to_broadcast([P, CHUNK, 2]))
-                elif t == 3 and c < 2:
+            for c in range(3):
+                src = windows[t][:, spans[c]]
+                if t == 2 and c == 0:
+                    nc.scalar.copy(out=grouped[c][:, :, 2:4], in_=src.unsqueeze(2).to_broadcast([P, 512, 2]))
+                elif t == 3 and c == 0:
                     nc.vector.tensor_copy(out=grouped[c][:, :, t], in_=src)
                 else:
                     nc.scalar.copy(out=grouped[c][:, :, t], in_=src)
@@ -145,16 +173,14 @@ def tile_picked_wema_none_lo_kernel(
         y_plane = keep.tile([P, U], U8, name="y_plane", align_bytes=64)
         y_codes = keep.tile([P, U], I32, name="y_codes", align_bytes=64)
         words_out = out_1[0].rearrange("p n t -> p (n t)").bitcast(I32)
-        for c in range(CHUNKS):
-            cols = slice(c * CHUNK, (c + 1) * CHUNK)
+        for c in (1, 0, 2):
+            cols = spans[c]
             nc.vector.quantize_mx(
                 out=y_codes[:, cols].bitcast(FP8X4),
                 scales=y_plane[:, cols],
                 in_=grouped[c][:].rearrange("p c t -> p (c t)"),
             )
-            if c > 0:
-                stored = slice(0, 2 * CHUNK) if c == 1 else cols
-                nc.sync.dma_start(words_out[:, stored], y_codes[:, stored])
+            nc.sync.dma_start(words_out[:, cols], y_codes[:, cols])
         for q in range(4):
             queue = nc.sync if q % 2 else nc.scalar
             queue.dma_start(

@@ -6,9 +6,9 @@ from concourse.masks import make_identity
 K, T, N, U = 512, 512, 512, 1024
 P = 128
 PACK = 4
-BLOCKS = T // P
-CHUNKS = 4
-CHUNK = U // CHUNKS
+HALF = T // 2
+SCATTER_MOST = 384
+VECTOR_SHARE = 128
 FLOPS = 2 * K * N * T
 
 F32 = mybir.dt.float32
@@ -30,155 +30,187 @@ def tile_picked_wema_none_lo_kernel(
     mem_rows = mem.rearrange("(p t) u -> p t u", t=PACK)
     out_rows = out_0.rearrange("(p t) u -> p t u", t=PACK)
     w_rows = w1.rearrange("(p j) c -> p j c", j=PACK)
+    x_flat = x_words[0].rearrange("p n t -> p (n t)").bitcast(I32)
+    first, second = slice(0, HALF), slice(HALF, T)
 
     with ExitStack() as ctx:
         keep = ctx.enter_context(tc.tile_pool(name="keep", bufs=1))
         psum = ctx.enter_context(tc.psum_pool(name="psum", bufs=1))
 
         offsets = keep.tile([P, T // 16], U16, name="offsets")
-        old_sb = keep.tile([P, T], F32, name="old_sb")
-        new_rows = keep.tile([P, P], F32, name="new_rows")
         windows = [keep.tile([P, U], F32, name="window%d" % t) for t in range(PACK)]
         w_raw = [keep.tile([P, 2, N], F32, name="w_raw%d" % h) for h in range(2)]
         x_codes = keep.tile([P, T], I32, name="x_codes", align_bytes=64)
         x_plane = keep.tile([P, T], U8, name="x_plane", align_bytes=64)
         ident = keep.tile([P, P], F32, name="ident")
+        old_col = keep.tile([P, PACK], F32, name="old_col")
+        new_col = keep.tile([P, PACK], F32, name="new_col")
 
-        nc.gpsimd.memset(new_rows[:], 0.0)
+        def listed(window, entries):
+            return window[:].indirect(offsets[:, entries.start // 16 : entries.stop // 16])
+
         nc.gpsimd.memset(x_plane[:].bitcast(I32), 0)
         make_identity(nc, ident[:])
 
-        old_col = keep.tile([P, PACK], F32, name="old_col")
-        nc.sync.dma_start(w_raw[0][:], w_rows[:, 0:2, :])
+        nc.sync.dma_start(new_col[:], new[0].rearrange("(p i) -> p i", i=PACK))
         nc.sync.dma_start(old_col[:], old[0].rearrange("(p i) -> p i", i=PACK))
-        nc.sync.dma_start(offsets[:], slot)
-        nc.sync.dma_start(new_rows[0:BLOCKS, :], new[0].rearrange("(b i) -> b i", b=BLOCKS))
-        nc.sync.dma_start(w_raw[1][:], w_rows[:, 2:4, :])
-        nc.sync.dma_start(windows[0][:], mem_rows[:, 0, :])
-        nc.sync.dma_start(x_codes[:], x_words[0].rearrange("p n t -> p (n t)").bitcast(I32))
+        nc.sync.dma_start(w_raw[0][:], w_rows[:, 0:2, :])
         for q in range(4):
             nc.sync.dma_start(
                 x_plane[32 * q : 32 * q + 4, :].bitcast(I32), x_scales[0, 4 * q : 4 * q + 4, :].bitcast(I32)
             )
+        nc.sync.dma_start(w_raw[1][:], w_rows[:, 2:4, :])
+        nc.sync.dma_start(x_codes[:], x_flat)
+        nc.sync.dma_start(windows[0][:], mem_rows[:, 0, :])
+        nc.sync.dma_start(offsets[:], slot)
         for t in range(1, PACK):
             nc.sync.dma_start(windows[t][:], mem_rows[:, t, :])
 
-        old_spread = psum.tile([P, PACK, P], F32, name="old_spread", tag="turn2")
-        for i in range(PACK):
-            nc.tensor.transpose(old_spread[:, i, :], old_col[:, i : i + 1].to_broadcast([P, P]), ident[:])
-        nc.scalar.activation(
-            old_sb[:].rearrange("q (p i) -> q p i", i=PACK), old_spread[:].rearrange("q i p -> q p i"), COPY
-        )
+        def spread(column, name):
+            turned = psum.tile([P, PACK, P], F32, name="turned", tag="bank_" + name)
+            for i in range(PACK):
+                nc.tensor.transpose(turned[:, i, :], column[:, i : i + 1].to_broadcast([P, P]), ident[:])
+            row = keep.tile([P, T], F32, name=name + "_row")
+            nc.scalar.activation(
+                row[:].rearrange("q (p i) -> q p i", i=PACK), turned[:].rearrange("q i p -> q p i"), COPY
+            )
+            return row
 
-        new_turned = psum.tile([P, P], F32, name="new_turned", tag="turn3")
-        nc.tensor.transpose(new_turned[:], new_rows[:], ident[:])
-        new_col = keep.tile([P, BLOCKS], F32, name="new_col")
-        nc.scalar.activation(new_col[:], new_turned[:, 0:BLOCKS], COPY)
-
-        kept = []
-        fresh = [keep.tile([P, T], F32, name="fresh%d" % t) for t in range(PACK)]
-
-        def gather(t):
-            looked_up = keep.tile([P, T], F32, name="looked_up", tag="kept%d" % (t % 3))
-            nc.vector.tensor_tensor(looked_up[:], windows[t][:].indirect(offsets[:]), old_sb[:], MULT)
-            kept.append(looked_up)
+        new_row = spread(new_col, "new")
+        old_row = spread(old_col, "old")
 
         w_codes = keep.tile([P, N], U32, name="w_codes", align_bytes=64)
         w_plane = keep.tile([P, N], U8, name="w_plane", align_bytes=64)
-        w_grouped = keep.tile([P, PACK, P, PACK], BF16, name="w_grouped", align_bytes=64)
+        stages = [slice(0, 1), slice(1, PACK)]
+        w_grouped = [
+            keep.tile([P, ts.stop - ts.start, P, PACK], BF16, name="w_grouped", tag=tag, align_bytes=64)
+            for ts, tag in zip(stages, ("kept", "w_rest"))
+        ]
         for h in range(2):
-            nc.vector.tensor_copy(
-                out=w_grouped[:, :, :, 2 * h : 2 * h + 2].rearrange("p t m j -> p m t j"),
-                in_=w_raw[h][:].rearrange("p j (m t) -> p m t j", t=PACK),
-            )
-        stages = [slice(0, 1), slice(1, 3), slice(3, 4)]
-        for ts in stages:
+            for ts, tile in zip(stages, w_grouped):
+                nc.vector.tensor_copy(
+                    out=tile[:, :, :, 2 * h : 2 * h + 2].rearrange("p t m j -> p m t j"),
+                    in_=w_raw[h][:].rearrange("p j (m t) -> p m t j", t=PACK)[:, :, ts, :],
+                )
+        for ts, tile in zip(stages, w_grouped):
             cols = slice(ts.start * P, ts.stop * P)
             nc.vector.quantize_mx(
                 out=w_codes[:, cols].bitcast(FP8X4),
                 scales=w_plane[:, cols],
-                in_=w_grouped[:, ts, :, :].rearrange("p t m j -> p (t m j)"),
+                in_=tile[:].rearrange("p t m j -> p (t m j)"),
             )
 
-        def project(acc, b, ts):
-            rows = slice(b * P, (b + 1) * P)
-            cols = slice(ts.start * P, ts.stop * P)
+        def project(t, entries, bank):
+            acc = psum.tile([P, entries.stop - entries.start], F32, name="acc", tag=bank)
+            cols = slice(t * P, (t + 1) * P)
             nc.tensor.matmul_mx(
-                out=acc,
-                lhsT=x_codes[:, rows].bitcast(FP8X4),
-                lhsT_scale=x_plane[:, rows],
-                rhs=w_codes[:, cols].bitcast(FP8X4),
-                rhs_scale=w_plane[:, cols],
+                out=acc[:],
+                lhsT=w_codes[:, cols].bitcast(FP8X4),
+                lhsT_scale=w_plane[:, cols],
+                rhs=x_codes[:, entries].bitcast(FP8X4),
+                rhs_scale=x_plane[:, entries],
                 start=True,
                 stop=True,
             )
+            return acc
 
-        first = []
-        for b in range(BLOCKS):
-            acc = psum.tile([P, P], F32, name="acc_first", tag="lead%d" % b)
-            project(acc[:], b, stages[0])
-            scaled = keep.tile([P, P], F32, name="first%d" % b)
-            nc.scalar.activation(scaled[:], acc[:], COPY, scale=new_col[:, b : b + 1])
-            first.append(scaled)
-        for b in range(BLOCKS):
-            piece = psum.tile([P, P], F32, name="piece", tag="turn%d" % b)
-            nc.tensor.transpose(piece[:], first[b][:], ident[:])
-            nc.scalar.copy(out=fresh[0][:, b * P : (b + 1) * P], in_=piece[:])
+        whole = slice(0, T)
 
-        rest = []
-        for b in range(BLOCKS):
-            acc = psum.tile([P, PACK - 1, P], F32, name="acc_rest", tag="turn%d" % b)
-            project(acc[:, 0:2, :].rearrange("j t p -> j (t p)"), b, stages[1])
-            project(acc[:, 2, :], b, stages[2])
-            if b < BLOCKS - 1:
-                others = keep.tile([P, PACK - 1, P], F32, name="others%d" % b)
-                nc.scalar.activation(others[:], acc[:], COPY, scale=new_col[:, b : b + 1])
-                rest.append([others[:, i, :] for i in range(PACK - 1)])
-            else:
-                ones = []
-                for i in range(PACK - 1):
-                    one = keep.tile([P, P], F32, name="one", tag="stage%d" % i, align_bytes=64)
-                    nc.scalar.activation(one[:], acc[:, i, :], COPY, scale=new_col[:, b : b + 1])
-                    ones.append(one[:])
-                rest.append(ones)
-        for t in range(1, PACK):
-            back = psum.tile([P, T], F32, name="back", tag="lead%d" % t)
-            for b in range(BLOCKS):
-                nc.tensor.transpose(back[:, b * P : (b + 1) * P], rest[b][t - 1], ident[:])
-            nc.scalar.copy(out=fresh[t][:], in_=back[:])
+        moved = [keep.tile([P, T], F32, name="moved%d" % t) for t in range(PACK)]
 
-        spans = [slice(0, 512), slice(512, 768), slice(768, 1024)]
-        grouped = [
-            keep.tile(
-                [P, spans[c].stop - spans[c].start, PACK], BF16, name="grouped", tag="stage%d" % c, align_bytes=64
-            )
-            for c in range(3)
-        ]
-        for t in range(PACK - 1):
-            gather(t)
-        for t in range(PACK):
-            if t == PACK - 1:
-                gather(t)
-            nc.vector.tensor_tensor(windows[t][:].indirect(offsets[:]), kept[t][:], fresh[t][:], ADD)
+        def kept_tile(entries):
+            return keep.tile([P, entries.stop - entries.start], F32, name="kept", tag="kept", align_bytes=64)
+
+        def weigh_new(t, entries, bank, buffer):
+            acc = project(t, entries, "bank_" + bank)
+            fresh = keep.tile([P, entries.stop - entries.start], F32, name="fresh", tag="fresh_" + buffer)
+            nc.vector.tensor_tensor(fresh[:], acc[:], new_row[:, entries], MULT)
+            return fresh
+
+        def gather(t, entries):
+            kept = kept_tile(entries)
+            nc.vector.tensor_tensor(kept[:], listed(windows[t], entries), old_row[:, entries], MULT)
+            return kept
+
+        def add(t, entries, kept, fresh):
+            nc.vector.tensor_tensor(moved[t][:, entries], kept, fresh, ADD)
+
+        def scatter(t, entries):
+            nc.scalar.activation(listed(windows[t], entries), moved[t][:, entries], COPY)
+
+        plain = keep.tile([P, HALF], F32, name="plain")
+        lead = weigh_new(0, first, "new", "a")
+        kept = gather(0, first)
+        nc.scalar.activation(plain[:], listed(windows[0], second), COPY)
+        follow = weigh_new(0, second, "old", "b")
+        add(0, first, kept[:], lead[:])
+        scatter(0, first)
+        kept = kept_tile(second)
+        nc.vector.tensor_tensor(kept[:], plain[:], old_row[:, second], MULT)
+        fresh = weigh_new(1, whole, "new", "a")
+        add(0, second, kept[:], follow[:])
+        scatter(0, second)
+        nc.sync.dma_start(out_rows[:, 0, :], windows[0][:])
+        most, rest = slice(0, SCATTER_MOST), slice(SCATTER_MOST, T)
+        for t, bank, buffer in ((1, "old", "b"), (2, "new", "a")):
+            kept = gather(t, whole)
+            ahead = weigh_new(t + 1, whole, bank, buffer)
+            for entries in (most, rest):
+                add(t, entries, kept[:, entries], fresh[:, entries])
+            scatter(t, most)
+            fresh = ahead
+        for t in (1, 2):
+            scatter(t, rest)
             nc.sync.dma_start(out_rows[:, t, :], windows[t][:])
-            for c in range(3):
-                src = windows[t][:, spans[c]]
-                if t == 2 and c == 0:
-                    nc.scalar.copy(out=grouped[c][:, :, 2:4], in_=src.unsqueeze(2).to_broadcast([P, 512, 2]))
-                elif t == 3 and c == 0:
-                    nc.vector.tensor_copy(out=grouped[c][:, :, t], in_=src)
-                else:
-                    nc.scalar.copy(out=grouped[c][:, :, t], in_=src)
+        last = PACK - 1
+        own, other = slice(0, VECTOR_SHARE), slice(VECTOR_SHARE, T)
+        kept = gather(last, whole)
+        nc.vector.tensor_tensor(listed(windows[last], own), kept[:, own], fresh[:, own], ADD)
+        add(last, other, kept[:, other], fresh[:, other])
+        scatter(last, other)
+        nc.sync.dma_start(out_rows[:, last, :], windows[last][:])
+
+        spans = [slice(0, U // 2), slice(U // 2, U)]
+        pairs = [
+            keep.tile([P, 2, U // 2, 2], BF16, name="pairs", tag="kept", align_bytes=64),
+            keep.tile([P, 2, U // 2, 2], BF16, name="pairs", tag="fresh_a"),
+        ]
+
+        def round_rows(t, c):
+            return pairs[c][:, t // 2, :, t % 2], windows[t][:, spans[c]]
+
+        for t in (0, 1):
+            for c in range(2):
+                nc.vector.tensor_copy(*round_rows(t, c))
+        nc.vector.tensor_copy(*round_rows(2, 0))
+        nc.vector.tensor_copy(
+            out=pairs[1][:, 1, :, :], in_=windows[2][:, spans[1]].unsqueeze(2).to_broadcast([P, U // 2, 2])
+        )
+        nc.vector.tensor_copy(*round_rows(last, 0))
+        nc.scalar.copy(*round_rows(last, 1))
+
+        pieces = [(0, slice(0, 512)), (1, slice(0, 256)), (1, slice(256, 512))]
+        grouped = []
+        for c, cols in pieces:
+            tile = keep.tile([P, cols.stop - cols.start, PACK], BF16, name="grouped%d" % len(grouped), align_bytes=64)
+            word = I32 if c == 0 else U32
+            dst = tile[:].rearrange("p c t -> p (c t)").bitcast(word).rearrange("p (c h) -> p c h", h=2)
+            src = pairs[c][:].rearrange("p h c e -> p h (c e)").bitcast(word)[:, :, cols].rearrange("p h c -> p c h")
+            if c == 0:
+                nc.vector.tensor_copy(out=dst, in_=src)
+            else:
+                nc.scalar.copy(out=dst, in_=src)
+            grouped.append(tile)
 
         y_plane = keep.tile([P, U], U8, name="y_plane", align_bytes=64)
         y_codes = keep.tile([P, U], I32, name="y_codes", align_bytes=64)
         words_out = out_1[0].rearrange("p n t -> p (n t)").bitcast(I32)
-        for c in (1, 0, 2):
-            cols = spans[c]
+        for (c, part), tile in zip(pieces, grouped):
+            cols = slice(spans[c].start + part.start, spans[c].start + part.stop)
             nc.vector.quantize_mx(
                 out=y_codes[:, cols].bitcast(FP8X4),
                 scales=y_plane[:, cols],
-                in_=grouped[c][:].rearrange("p c t -> p (c t)"),
+                in_=tile[:].rearrange("p c t -> p (c t)"),
             )
             nc.sync.dma_start(words_out[:, cols], y_codes[:, cols])
         for q in range(4):

@@ -8,7 +8,6 @@ P = 128
 PACK = 4
 HALF = T // 2
 SCATTER_MOST = 384
-VECTOR_SHARE = 128
 FLOPS = 2 * K * N * T
 
 F32 = mybir.dt.float32
@@ -40,10 +39,10 @@ def tile_picked_wema_none_lo_kernel(
         offsets = keep.tile([P, T // 16], U16, name="offsets")
         windows = [keep.tile([P, U], F32, name="window%d" % t) for t in range(PACK)]
         w_raw = [keep.tile([P, 2, N], F32, name="w_raw%d" % h) for h in range(2)]
-        x_codes = keep.tile([P, T], I32, name="x_codes", align_bytes=64)
+        x_codes = [keep.tile([P, HALF], I32, name="x_codes%d" % h, align_bytes=64) for h in range(2)]
         x_plane = keep.tile([P, T], U8, name="x_plane", align_bytes=64)
         ident = keep.tile([P, P], F32, name="ident")
-        old_col = keep.tile([P, PACK], F32, name="old_col")
+        old_col = keep.tile([P, PACK], F32, name="old_col", tag="w_two", align_bytes=64)
         new_col = keep.tile([P, PACK], F32, name="new_col")
 
         def listed(window, entries):
@@ -54,15 +53,16 @@ def tile_picked_wema_none_lo_kernel(
 
         nc.sync.dma_start(new_col[:], new[0].rearrange("(p i) -> p i", i=PACK))
         nc.sync.dma_start(old_col[:], old[0].rearrange("(p i) -> p i", i=PACK))
-        nc.sync.dma_start(w_raw[0][:], w_rows[:, 0:2, :])
+        nc.sync.dma_start(offsets[:], slot)
+        for h in range(2):
+            nc.sync.dma_start(w_raw[h][:], w_rows[:, 2 * h : 2 * h + 2, :])
         for q in range(4):
             nc.sync.dma_start(
                 x_plane[32 * q : 32 * q + 4, :].bitcast(I32), x_scales[0, 4 * q : 4 * q + 4, :].bitcast(I32)
             )
-        nc.sync.dma_start(w_raw[1][:], w_rows[:, 2:4, :])
-        nc.sync.dma_start(x_codes[:], x_flat)
+        nc.sync.dma_start(x_codes[0][:], x_flat[:, first])
         nc.sync.dma_start(windows[0][:], mem_rows[:, 0, :])
-        nc.sync.dma_start(offsets[:], slot)
+        nc.sync.dma_start(x_codes[1][:], x_flat[:, second])
         for t in range(1, PACK):
             nc.sync.dma_start(windows[t][:], mem_rows[:, t, :])
 
@@ -79,56 +79,58 @@ def tile_picked_wema_none_lo_kernel(
         new_row = spread(new_col, "new")
         old_row = spread(old_col, "old")
 
-        w_codes = keep.tile([P, N], U32, name="w_codes", align_bytes=64)
-        w_plane = keep.tile([P, N], U8, name="w_plane", align_bytes=64)
-        stages = [slice(0, 1), slice(1, PACK)]
+        stages = [(slice(0, 1), nc.vector, "kept"), (slice(1, 2), nc.vector, "w_one"), (slice(2, 4), nc.scalar, "w_two")]
         w_grouped = [
             keep.tile([P, ts.stop - ts.start, P, PACK], BF16, name="w_grouped", tag=tag, align_bytes=64)
-            for ts, tag in zip(stages, ("kept", "w_rest"))
+            for ts, engine, tag in stages
         ]
         for h in range(2):
-            for ts, tile in zip(stages, w_grouped):
-                nc.vector.tensor_copy(
-                    out=tile[:, :, :, 2 * h : 2 * h + 2].rearrange("p t m j -> p m t j"),
-                    in_=w_raw[h][:].rearrange("p j (m t) -> p m t j", t=PACK)[:, :, ts, :],
-                )
-        for ts, tile in zip(stages, w_grouped):
-            cols = slice(ts.start * P, ts.stop * P)
+            for (ts, engine, tag), tile in zip(stages, w_grouped):
+                dst = tile[:, :, :, 2 * h : 2 * h + 2].rearrange("p t m j -> p m t j")
+                src = w_raw[h][:].rearrange("p j (m t) -> p m t j", t=PACK)[:, :, ts, :]
+                if ts.start < 2:
+                    nc.vector.tensor_copy(out=dst, in_=src)
+                else:
+                    nc.scalar.copy(out=dst, in_=src)
+        stationary = []
+        for (ts, engine, tag), tile in zip(stages, w_grouped):
+            width = (ts.stop - ts.start) * P
+            codes = keep.tile([P, width], U32, name="w_codes%d" % ts.start, align_bytes=64)
+            plane = keep.tile([P, width], U8, name="w_plane%d" % ts.start, align_bytes=64)
             nc.vector.quantize_mx(
-                out=w_codes[:, cols].bitcast(FP8X4),
-                scales=w_plane[:, cols],
-                in_=tile[:].rearrange("p t m j -> p (t m j)"),
+                out=codes[:].bitcast(FP8X4), scales=plane[:], in_=tile[:].rearrange("p t m j -> p (t m j)")
             )
+            for i in range(0, width, P):
+                stationary.append((codes[:, i : i + P], plane[:, i : i + P]))
 
         def project(t, entries, bank):
             acc = psum.tile([P, entries.stop - entries.start], F32, name="acc", tag=bank)
-            cols = slice(t * P, (t + 1) * P)
-            nc.tensor.matmul_mx(
-                out=acc[:],
-                lhsT=w_codes[:, cols].bitcast(FP8X4),
-                lhsT_scale=w_plane[:, cols],
-                rhs=x_codes[:, entries].bitcast(FP8X4),
-                rhs_scale=x_plane[:, entries],
-                start=True,
-                stop=True,
-            )
+            for h in range(entries.start // HALF, entries.stop // HALF):
+                nc.tensor.matmul_mx(
+                    out=acc[:, h * HALF - entries.start : (h + 1) * HALF - entries.start],
+                    lhsT=stationary[t][0].bitcast(FP8X4),
+                    lhsT_scale=stationary[t][1],
+                    rhs=x_codes[h][:].bitcast(FP8X4),
+                    rhs_scale=x_plane[:, h * HALF : (h + 1) * HALF],
+                    start=True,
+                    stop=True,
+                )
             return acc
 
         whole = slice(0, T)
-
         moved = [keep.tile([P, T], F32, name="moved%d" % t) for t in range(PACK)]
 
-        def kept_tile(entries):
-            return keep.tile([P, entries.stop - entries.start], F32, name="kept", tag="kept", align_bytes=64)
+        def buffer(entries, tag):
+            return keep.tile([P, entries.stop - entries.start], F32, name="buffer", tag=tag, align_bytes=64)
 
-        def weigh_new(t, entries, bank, buffer):
+        def weigh_new(t, entries, bank, tag):
             acc = project(t, entries, "bank_" + bank)
-            fresh = keep.tile([P, entries.stop - entries.start], F32, name="fresh", tag="fresh_" + buffer)
+            fresh = buffer(entries, tag)
             nc.vector.tensor_tensor(fresh[:], acc[:], new_row[:, entries], MULT)
             return fresh
 
-        def gather(t, entries):
-            kept = kept_tile(entries)
+        def gather(t, entries, tag):
+            kept = buffer(entries, tag)
             nc.vector.tensor_tensor(kept[:], listed(windows[t], entries), old_row[:, entries], MULT)
             return kept
 
@@ -138,56 +140,62 @@ def tile_picked_wema_none_lo_kernel(
         def scatter(t, entries):
             nc.scalar.activation(listed(windows[t], entries), moved[t][:, entries], COPY)
 
-        plain = keep.tile([P, HALF], F32, name="plain")
-        lead = weigh_new(0, first, "new", "a")
-        kept = gather(0, first)
-        nc.scalar.activation(plain[:], listed(windows[0], second), COPY)
-        follow = weigh_new(0, second, "old", "b")
-        add(0, first, kept[:], lead[:])
-        scatter(0, first)
-        kept = kept_tile(second)
-        nc.vector.tensor_tensor(kept[:], plain[:], old_row[:, second], MULT)
-        fresh = weigh_new(1, whole, "new", "a")
-        add(0, second, kept[:], follow[:])
-        scatter(0, second)
-        nc.sync.dma_start(out_rows[:, 0, :], windows[0][:])
-        most, rest = slice(0, SCATTER_MOST), slice(SCATTER_MOST, T)
-        for t, bank, buffer in ((1, "old", "b"), (2, "new", "a")):
-            kept = gather(t, whole)
-            ahead = weigh_new(t + 1, whole, bank, buffer)
-            for entries in (most, rest):
-                add(t, entries, kept[:, entries], fresh[:, entries])
-            scatter(t, most)
-            fresh = ahead
-        for t in (1, 2):
-            scatter(t, rest)
+        def scatter_sum(t, entries, kept, fresh):
+            nc.vector.tensor_tensor(listed(windows[t], entries), kept, fresh, ADD)
+
+        def store(t):
             nc.sync.dma_start(out_rows[:, t, :], windows[t][:])
-        last = PACK - 1
-        own, other = slice(0, VECTOR_SHARE), slice(VECTOR_SHARE, T)
-        kept = gather(last, whole)
-        nc.vector.tensor_tensor(listed(windows[last], own), kept[:, own], fresh[:, own], ADD)
-        add(last, other, kept[:, other], fresh[:, other])
-        scatter(last, other)
-        nc.sync.dma_start(out_rows[:, last, :], windows[last][:])
 
         spans = [slice(0, U // 2), slice(U // 2, U)]
-        pairs = [
-            keep.tile([P, 2, U // 2, 2], BF16, name="pairs", tag="kept", align_bytes=64),
-            keep.tile([P, 2, U // 2, 2], BF16, name="pairs", tag="fresh_a"),
-        ]
+        pairs = {}
 
         def round_rows(t, c):
+            if c not in pairs:
+                tag = ("one", "three")[c]
+                pairs.setdefault(c, keep.tile([P, 2, U // 2, 2], BF16, name="pairs", tag=tag, align_bytes=64))
             return pairs[c][:, t // 2, :, t % 2], windows[t][:, spans[c]]
 
-        for t in (0, 1):
-            for c in range(2):
-                nc.vector.tensor_copy(*round_rows(t, c))
-        nc.vector.tensor_copy(*round_rows(2, 0))
-        nc.vector.tensor_copy(
-            out=pairs[1][:, 1, :, :], in_=windows[2][:, spans[1]].unsqueeze(2).to_broadcast([P, U // 2, 2])
-        )
-        nc.vector.tensor_copy(*round_rows(last, 0))
-        nc.scalar.copy(*round_rows(last, 1))
+        most, rest = slice(0, SCATTER_MOST), slice(SCATTER_MOST, T)
+        plain = keep.tile([P, HALF], F32, name="plain")
+        fresh_0a = weigh_new(0, first, "new", "lead")
+        kept_0a = gather(0, first, "kept")
+        nc.scalar.activation(plain[:], listed(windows[0], second), COPY)
+        kept_0b = buffer(second, "follow")
+        nc.vector.tensor_tensor(kept_0b[:], plain[:], old_row[:, second], MULT)
+        add(0, first, kept_0a[:], fresh_0a[:])
+        scatter(0, first)
+        fresh_1 = weigh_new(1, whole, "new", "one")
+        fresh_0b = weigh_new(0, second, "old", "lead")
+        kept_1 = gather(1, most, "kept")
+        add(0, second, kept_0b[:], fresh_0b[:])
+        scatter(0, second)
+        store(0)
+        add(1, most, kept_1[:], fresh_1[:, most])
+        scatter(1, most)
+        kept_2 = gather(2, most, "follow")
+        fresh_2 = weigh_new(2, whole, "old", "lead")
+        kept_3 = gather(3, whole, "kept")
+        add(2, most, kept_2[:], fresh_2[:, most])
+        scatter(2, most)
+        fresh_3 = weigh_new(3, whole, "old", "three")
+        kept_1 = gather(1, rest, "follow")
+        scatter_sum(3, rest, kept_3[:, rest], fresh_3[:, rest])
+        add(3, most, kept_3[:, most], fresh_3[:, most])
+        scatter(3, most)
+        store(3)
+        scatter_sum(1, rest, kept_1[:], fresh_1[:, rest])
+        store(1)
+        kept_2 = gather(2, rest, "kept")
+        nc.vector.tensor_copy(*round_rows(0, 1))
+        scatter_sum(2, rest, kept_2[:], fresh_2[:, rest])
+        store(2)
+
+        nc.vector.tensor_copy(*round_rows(0, 0))
+        for c in (1, 0):
+            nc.vector.tensor_copy(*round_rows(1, c))
+        for t in (2, 3):
+            nc.vector.tensor_copy(*round_rows(t, 0))
+            nc.scalar.copy(*round_rows(t, 1))
 
         pieces = [(0, slice(0, 512)), (1, slice(0, 256)), (1, slice(256, 512))]
         grouped = []

@@ -7,7 +7,6 @@ K, T, N, U = 512, 512, 512, 1024
 P = 128
 PACK = 4
 HALF = T // 2
-SCATTER_MOST = 384
 FLOPS = 2 * K * N * T
 
 F32 = mybir.dt.float32
@@ -42,7 +41,7 @@ def tile_picked_wema_none_lo_kernel(
         x_codes = [keep.tile([P, HALF], I32, name="x_codes%d" % h, align_bytes=64) for h in range(2)]
         x_plane = keep.tile([P, T], U8, name="x_plane", align_bytes=64)
         ident = keep.tile([P, P], F32, name="ident")
-        old_col = keep.tile([P, PACK], F32, name="old_col", tag="w_two", align_bytes=64)
+        old_col = keep.tile([P, PACK], F32, name="old_col", tag="old_col", align_bytes=64)
         new_col = keep.tile([P, PACK], F32, name="new_col")
 
         def listed(window, entries):
@@ -62,8 +61,9 @@ def tile_picked_wema_none_lo_kernel(
             )
         nc.sync.dma_start(x_codes[0][:], x_flat[:, first])
         nc.sync.dma_start(windows[0][:], mem_rows[:, 0, :])
+        nc.sync.dma_start(windows[1][:], mem_rows[:, 1, :])
         nc.sync.dma_start(x_codes[1][:], x_flat[:, second])
-        for t in range(1, PACK):
+        for t in (2, 3):
             nc.sync.dma_start(windows[t][:], mem_rows[:, t, :])
 
         def spread(column, name):
@@ -79,66 +79,73 @@ def tile_picked_wema_none_lo_kernel(
         new_row = spread(new_col, "new")
         old_row = spread(old_col, "old")
 
-        stages = [(slice(0, 1), nc.vector, "kept"), (slice(1, 2), nc.vector, "w_one"), (slice(2, 4), nc.scalar, "w_two")]
-        w_grouped = [
-            keep.tile([P, ts.stop - ts.start, P, PACK], BF16, name="w_grouped", tag=tag, align_bytes=64)
-            for ts, engine, tag in stages
-        ]
+        w_low = keep.tile([P, 2, P, PACK], BF16, name="w_low", align_bytes=64)
+        w_high = keep.tile([P, 2, P, PACK], BF16, name="w_high", tag="old_col", align_bytes=64)
         for h in range(2):
-            for (ts, engine, tag), tile in zip(stages, w_grouped):
-                dst = tile[:, :, :, 2 * h : 2 * h + 2].rearrange("p t m j -> p m t j")
-                src = w_raw[h][:].rearrange("p j (m t) -> p m t j", t=PACK)[:, :, ts, :]
-                if ts.start < 2:
-                    nc.vector.tensor_copy(out=dst, in_=src)
-                else:
-                    nc.scalar.copy(out=dst, in_=src)
+            src = w_raw[h][:].rearrange("p j (m t) -> p m t j", t=PACK)
+            nc.vector.tensor_copy(
+                out=w_low[:, :, :, 2 * h : 2 * h + 2].rearrange("p t m j -> p m t j"), in_=src[:, :, 0:2, :]
+            )
+            nc.scalar.copy(
+                out=w_high[:, :, :, 2 * h : 2 * h + 2].rearrange("p t m j -> p m t j"), in_=src[:, :, 2:4, :]
+            )
         stationary = []
-        for (ts, engine, tag), tile in zip(stages, w_grouped):
-            width = (ts.stop - ts.start) * P
-            codes = keep.tile([P, width], U32, name="w_codes%d" % ts.start, align_bytes=64)
-            plane = keep.tile([P, width], U8, name="w_plane%d" % ts.start, align_bytes=64)
+        for grouped_w in (w_low[:, 0:1], w_low[:, 1:2], w_high[:]):
+            width = grouped_w.shape[1] * P
+            codes = keep.tile([P, width], U32, name="w_codes%d" % len(stationary), align_bytes=64)
+            plane = keep.tile([P, width], U8, name="w_plane%d" % len(stationary), align_bytes=64)
             nc.vector.quantize_mx(
-                out=codes[:].bitcast(FP8X4), scales=plane[:], in_=tile[:].rearrange("p t m j -> p (t m j)")
+                out=codes[:].bitcast(FP8X4), scales=plane[:], in_=grouped_w.rearrange("p t m j -> p (t m j)")
             )
             for i in range(0, width, P):
                 stationary.append((codes[:, i : i + P], plane[:, i : i + P]))
 
+        halves = [first, second]
+
+        def buffer(tag, width=HALF):
+            return keep.tile([P, width], F32, name="buffer", tag=tag, align_bytes=64)
+
         def project(t, entries, bank):
-            acc = psum.tile([P, entries.stop - entries.start], F32, name="acc", tag=bank)
+            acc = psum.tile([P, entries.stop - entries.start], F32, name="acc", tag="bank_" + bank)
             for h in range(entries.start // HALF, entries.stop // HALF):
                 nc.tensor.matmul_mx(
                     out=acc[:, h * HALF - entries.start : (h + 1) * HALF - entries.start],
                     lhsT=stationary[t][0].bitcast(FP8X4),
                     lhsT_scale=stationary[t][1],
                     rhs=x_codes[h][:].bitcast(FP8X4),
-                    rhs_scale=x_plane[:, h * HALF : (h + 1) * HALF],
+                    rhs_scale=x_plane[:, halves[h]],
                     start=True,
                     stop=True,
                 )
             return acc
 
-        whole = slice(0, T)
-        moved = [keep.tile([P, T], F32, name="moved%d" % t) for t in range(PACK)]
-
-        def buffer(entries, tag):
-            return keep.tile([P, entries.stop - entries.start], F32, name="buffer", tag=tag, align_bytes=64)
-
-        def weigh_new(t, entries, bank, tag):
-            acc = project(t, entries, "bank_" + bank)
-            fresh = buffer(entries, tag)
-            nc.vector.tensor_tensor(fresh[:], acc[:], new_row[:, entries], MULT)
+        def weigh(acc, entries, tag):
+            fresh = buffer(tag, entries.stop - entries.start)
+            nc.vector.tensor_tensor(fresh[:], acc, new_row[:, entries], MULT)
             return fresh
 
+        def weigh_new(t, entries, bank, tag):
+            return weigh(project(t, entries, bank)[:], entries, tag)
+
+        def look_up(t, h, tag):
+            plain = buffer(tag)
+            nc.scalar.activation(plain[:], listed(windows[t], halves[h]), COPY)
+            return plain
+
+        def weigh_old(plain, h, tag):
+            kept = buffer(tag)
+            nc.vector.tensor_tensor(kept[:], plain[:], old_row[:, halves[h]], MULT)
+            return kept
+
         def gather(t, entries, tag):
-            kept = buffer(entries, tag)
+            kept = buffer(tag, entries.stop - entries.start)
             nc.vector.tensor_tensor(kept[:], listed(windows[t], entries), old_row[:, entries], MULT)
             return kept
 
-        def add(t, entries, kept, fresh):
-            nc.vector.tensor_tensor(moved[t][:, entries], kept, fresh, ADD)
-
-        def scatter(t, entries):
-            nc.scalar.activation(listed(windows[t], entries), moved[t][:, entries], COPY)
+        def add_and_scatter(t, entries, kept, fresh, tag):
+            moved = buffer(tag, entries.stop - entries.start)
+            nc.vector.tensor_tensor(moved[:], kept, fresh, ADD)
+            nc.scalar.activation(listed(windows[t], entries), moved[:], COPY)
 
         def scatter_sum(t, entries, kept, fresh):
             nc.vector.tensor_tensor(listed(windows[t], entries), kept, fresh, ADD)
@@ -146,65 +153,60 @@ def tile_picked_wema_none_lo_kernel(
         def store(t):
             nc.sync.dma_start(out_rows[:, t, :], windows[t][:])
 
-        spans = [slice(0, U // 2), slice(U // 2, U)]
-        pairs = {}
+        whole = slice(0, T)
 
-        def round_rows(t, c):
-            if c not in pairs:
-                tag = ("one", "three")[c]
-                pairs.setdefault(c, keep.tile([P, 2, U // 2, 2], BF16, name="pairs", tag=tag, align_bytes=64))
-            return pairs[c][:, t // 2, :, t % 2], windows[t][:, spans[c]]
-
-        most, rest = slice(0, SCATTER_MOST), slice(SCATTER_MOST, T)
-        plain = keep.tile([P, HALF], F32, name="plain")
-        fresh_0a = weigh_new(0, first, "new", "lead")
-        kept_0a = gather(0, first, "kept")
-        nc.scalar.activation(plain[:], listed(windows[0], second), COPY)
-        kept_0b = buffer(second, "follow")
-        nc.vector.tensor_tensor(kept_0b[:], plain[:], old_row[:, second], MULT)
-        add(0, first, kept_0a[:], fresh_0a[:])
-        scatter(0, first)
-        fresh_1 = weigh_new(1, whole, "new", "one")
-        fresh_0b = weigh_new(0, second, "old", "lead")
-        kept_1 = gather(1, most, "kept")
-        add(0, second, kept_0b[:], fresh_0b[:])
-        scatter(0, second)
+        plain_0b = look_up(0, 1, "plain_0b")
+        plain_1a = look_up(1, 0, "plain_1a")
+        plain_1b = look_up(1, 1, "plain_1b")
+        fresh_0a = weigh_new(0, first, "new", "fresh_0a")
+        kept_0a = gather(0, first, "kept_0a")
+        fresh_1a = weigh_new(1, first, "old", "fresh_1a")
+        add_and_scatter(0, first, kept_0a[:], fresh_0a[:], "moved_0a")
+        kept_1a = weigh_old(plain_1a, 0, "kept_0a")
+        kept_0b = weigh_old(plain_0b, 1, "fresh_0a")
+        add_and_scatter(1, first, kept_1a[:], fresh_1a[:], "moved_1a")
+        fresh_0b = weigh_new(0, second, "new", "plain_1a")
+        kept_1b = weigh_old(plain_1b, 1, "plain_0b")
+        fresh_1b = weigh_new(1, second, "old", "fresh_1a")
+        add_and_scatter(0, second, kept_0b[:], fresh_0b[:], "moved_0b")
         store(0)
-        add(1, most, kept_1[:], fresh_1[:, most])
-        scatter(1, most)
-        kept_2 = gather(2, most, "follow")
-        fresh_2 = weigh_new(2, whole, "old", "lead")
-        kept_3 = gather(3, whole, "kept")
-        add(2, most, kept_2[:], fresh_2[:, most])
-        scatter(2, most)
-        fresh_3 = weigh_new(3, whole, "old", "three")
-        kept_1 = gather(1, rest, "follow")
-        scatter_sum(3, rest, kept_3[:, rest], fresh_3[:, rest])
-        add(3, most, kept_3[:, most], fresh_3[:, most])
-        scatter(3, most)
-        store(3)
-        scatter_sum(1, rest, kept_1[:], fresh_1[:, rest])
+        kept_2 = gather(2, whole, "plain_1b")
+        add_and_scatter(1, second, kept_1b[:], fresh_1b[:], "moved_1b")
         store(1)
-        kept_2 = gather(2, rest, "kept")
-        nc.vector.tensor_copy(*round_rows(0, 1))
-        scatter_sum(2, rest, kept_2[:], fresh_2[:, rest])
+        fresh_2 = weigh_new(2, whole, "two", "fresh_0a")
+        kept_3 = gather(3, whole, "plain_1a")
+        fresh_3 = weigh_new(3, whole, "three", "plain_0b")
+        add_and_scatter(2, first, kept_2[:, first], fresh_2[:, first], "moved_2a")
+        scatter_sum(3, second, kept_3[:, second], fresh_3[:, second])
+        add_and_scatter(3, first, kept_3[:, first], fresh_3[:, first], "moved_3a")
+        store(3)
+        add_and_scatter(2, second, kept_2[:, second], fresh_2[:, second], "plain_0b")
         store(2)
 
-        nc.vector.tensor_copy(*round_rows(0, 0))
-        for c in (1, 0):
-            nc.vector.tensor_copy(*round_rows(1, c))
-        for t in (2, 3):
-            nc.vector.tensor_copy(*round_rows(t, 0))
-            nc.scalar.copy(*round_rows(t, 1))
+        spans = [slice(0, 384), slice(384, 640), slice(640, U)]
+        pairs = [
+            keep.tile([P, 2, span.stop - span.start, 2], BF16, name="pairs", tag=tag, align_bytes=64)
+            for span, tag in zip(spans, ("plain_1b", "plain_1a", "fresh_0a"))
+        ]
+        for t in range(2):
+            for span, tile in zip(spans, pairs):
+                nc.vector.tensor_copy(out=tile[:, 0, :, t], in_=windows[t][:, span])
+        shared = spans[2].stop - spans[2].start
+        nc.vector.tensor_copy(
+            out=pairs[2][:, 1, :, :], in_=windows[3][:, spans[2]].unsqueeze(2).to_broadcast([P, shared, 2])
+        )
+        for t in (3, 2):
+            for c in range(2):
+                nc.vector.tensor_copy(out=pairs[c][:, 1, :, t % 2], in_=windows[t][:, spans[c]])
+        nc.scalar.copy(out=pairs[2][:, 1, :, 0], in_=windows[2][:, spans[2]])
 
-        pieces = [(0, slice(0, 512)), (1, slice(0, 256)), (1, slice(256, 512))]
         grouped = []
-        for c, cols in pieces:
-            tile = keep.tile([P, cols.stop - cols.start, PACK], BF16, name="grouped%d" % len(grouped), align_bytes=64)
-            word = I32 if c == 0 else U32
+        for c, span in enumerate(spans):
+            tile = keep.tile([P, span.stop - span.start, PACK], BF16, name="grouped%d" % c, align_bytes=64)
+            word = I32 if c < 2 else U32
             dst = tile[:].rearrange("p c t -> p (c t)").bitcast(word).rearrange("p (c h) -> p c h", h=2)
-            src = pairs[c][:].rearrange("p h c e -> p h (c e)").bitcast(word)[:, :, cols].rearrange("p h c -> p c h")
-            if c == 0:
+            src = pairs[c][:].rearrange("p h c e -> p h (c e)").bitcast(word).rearrange("p h c -> p c h")
+            if c < 2:
                 nc.vector.tensor_copy(out=dst, in_=src)
             else:
                 nc.scalar.copy(out=dst, in_=src)
@@ -213,14 +215,13 @@ def tile_picked_wema_none_lo_kernel(
         y_plane = keep.tile([P, U], U8, name="y_plane", align_bytes=64)
         y_codes = keep.tile([P, U], I32, name="y_codes", align_bytes=64)
         words_out = out_1[0].rearrange("p n t -> p (n t)").bitcast(I32)
-        for (c, part), tile in zip(pieces, grouped):
-            cols = slice(spans[c].start + part.start, spans[c].start + part.stop)
+        for span, tile in zip(spans, grouped):
             nc.vector.quantize_mx(
-                out=y_codes[:, cols].bitcast(FP8X4),
-                scales=y_plane[:, cols],
+                out=y_codes[:, span].bitcast(FP8X4),
+                scales=y_plane[:, span],
                 in_=tile[:].rearrange("p c t -> p (c t)"),
             )
-            nc.sync.dma_start(words_out[:, cols], y_codes[:, cols])
+            nc.sync.dma_start(words_out[:, span], y_codes[:, span])
         for q in range(4):
             queue = nc.sync if q % 2 else nc.scalar
             queue.dma_start(

@@ -7,6 +7,7 @@ K, T, N, U = 512, 512, 512, 1024
 P = 128
 PACK = 4
 HALF = T // 2
+SPLIT = 448
 FLOPS = 2 * K * N * T
 
 F32 = mybir.dt.float32
@@ -155,11 +156,12 @@ def tile_picked_wema_none_lo_kernel(
 
         whole = slice(0, T)
 
+        plain_0a = look_up(0, 0, "plain_0a")
         plain_0b = look_up(0, 1, "plain_0b")
         plain_1a = look_up(1, 0, "plain_1a")
         plain_1b = look_up(1, 1, "plain_1b")
         fresh_0a = weigh_new(0, first, "new", "fresh_0a")
-        kept_0a = gather(0, first, "kept_0a")
+        kept_0a = weigh_old(plain_0a, 0, "kept_0a")
         fresh_1a = weigh_new(1, first, "old", "fresh_1a")
         add_and_scatter(0, first, kept_0a[:], fresh_0a[:], "moved_0a")
         kept_1a = weigh_old(plain_1a, 0, "kept_0a")
@@ -173,41 +175,47 @@ def tile_picked_wema_none_lo_kernel(
         kept_2 = gather(2, whole, "plain_1b")
         add_and_scatter(1, second, kept_1b[:], fresh_1b[:], "moved_1b")
         store(1)
-        fresh_2 = weigh_new(2, whole, "two", "fresh_0a")
+        scalar_part, vector_part = slice(0, SPLIT), slice(SPLIT, T)
+        acc_2 = project(2, whole, "two")
+        fresh_2 = weigh(acc_2[:, scalar_part], scalar_part, "fresh_0a")
         kept_3 = gather(3, whole, "plain_1a")
         fresh_3 = weigh_new(3, whole, "three", "plain_0b")
         add_and_scatter(2, first, kept_2[:, first], fresh_2[:, first], "moved_2a")
         scatter_sum(3, second, kept_3[:, second], fresh_3[:, second])
         add_and_scatter(3, first, kept_3[:, first], fresh_3[:, first], "moved_3a")
         store(3)
-        add_and_scatter(2, second, kept_2[:, second], fresh_2[:, second], "plain_0b")
+        fresh_2c = weigh(acc_2[:, vector_part], vector_part, "plain_1a")
+        scatter_sum(2, vector_part, kept_2[:, vector_part], fresh_2c[:])
+        ending = slice(HALF, SPLIT)
+        add_and_scatter(2, ending, kept_2[:, ending], fresh_2[:, ending], "plain_0b")
         store(2)
 
         spans = [slice(0, 384), slice(384, 640), slice(640, U)]
+        sides = [slice(0, 640), slice(640, U)]
         pairs = [
-            keep.tile([P, 2, span.stop - span.start, 2], BF16, name="pairs", tag=tag, align_bytes=64)
-            for span, tag in zip(spans, ("plain_1b", "plain_1a", "fresh_0a"))
+            keep.tile([P, 2, side.stop - side.start, 2], BF16, name="pairs", tag=tag, align_bytes=64)
+            for side, tag in zip(sides, ("plain_1b", "fresh_0a"))
         ]
         for t in range(2):
-            for span, tile in zip(spans, pairs):
-                nc.vector.tensor_copy(out=tile[:, 0, :, t], in_=windows[t][:, span])
-        shared = spans[2].stop - spans[2].start
+            for side, tile in zip(sides, pairs):
+                nc.vector.tensor_copy(out=tile[:, 0, :, t], in_=windows[t][:, side])
+        shared = sides[1].stop - sides[1].start
         nc.vector.tensor_copy(
-            out=pairs[2][:, 1, :, :], in_=windows[3][:, spans[2]].unsqueeze(2).to_broadcast([P, shared, 2])
+            out=pairs[1][:, 1, :, :], in_=windows[3][:, sides[1]].unsqueeze(2).to_broadcast([P, shared, 2])
         )
-        for t in (3, 2):
-            for c in range(2):
-                nc.vector.tensor_copy(out=pairs[c][:, 1, :, t % 2], in_=windows[t][:, spans[c]])
-        nc.scalar.copy(out=pairs[2][:, 1, :, 0], in_=windows[2][:, spans[2]])
+        nc.vector.tensor_copy(out=pairs[0][:, 1, :, 1], in_=windows[3][:, sides[0]])
+        for span in spans[:2]:
+            nc.vector.tensor_copy(out=pairs[0][:, 1, span, 0], in_=windows[2][:, span])
+        nc.scalar.copy(out=pairs[1][:, 1, :, 0], in_=windows[2][:, sides[1]])
 
         grouped = []
         for c, span in enumerate(spans):
             tile = keep.tile([P, span.stop - span.start, PACK], BF16, name="grouped%d" % c, align_bytes=64)
             word = I32 if c < 2 else U32
             dst = tile[:].rearrange("p c t -> p (c t)").bitcast(word).rearrange("p (c h) -> p c h", h=2)
-            src = pairs[c][:].rearrange("p h c e -> p h (c e)").bitcast(word).rearrange("p h c -> p c h")
+            src = pairs[c // 2][:].rearrange("p h c e -> p h (c e)").bitcast(word).rearrange("p h c -> p c h")
             if c < 2:
-                nc.vector.tensor_copy(out=dst, in_=src)
+                nc.vector.tensor_copy(out=dst, in_=src[:, span, :])
             else:
                 nc.scalar.copy(out=dst, in_=src)
             grouped.append(tile)

@@ -7,7 +7,6 @@ K, T, N, U = 512, 512, 512, 1024
 P = 128
 PACK = 4
 HALF = T // 2
-SPLIT = 448
 FLOPS = 2 * K * N * T
 
 F32 = mybir.dt.float32
@@ -34,11 +33,12 @@ def tile_picked_wema_none_lo_kernel(
 
     with ExitStack() as ctx:
         keep = ctx.enter_context(tc.tile_pool(name="keep", bufs=1))
+        turns = ctx.enter_context(tc.tile_pool(name="turns", bufs=1))
         psum = ctx.enter_context(tc.psum_pool(name="psum", bufs=1))
 
         offsets = keep.tile([P, T // 16], U16, name="offsets")
         windows = [keep.tile([P, U], F32, name="window%d" % t) for t in range(PACK)]
-        w_raw = [keep.tile([P, 2, N], F32, name="w_raw%d" % h) for h in range(2)]
+        w_raw = [keep.tile([P, 2, N], F32, name="w_raw0"), turns.tile([P, 2, N], F32, name="w_raw1", offset=0, align_bytes=64)]
         x_codes = [keep.tile([P, HALF], I32, name="x_codes%d" % h, align_bytes=64) for h in range(2)]
         x_plane = keep.tile([P, T], U8, name="x_plane", align_bytes=64)
         ident = keep.tile([P, P], F32, name="ident")
@@ -48,7 +48,6 @@ def tile_picked_wema_none_lo_kernel(
         def listed(window, entries):
             return window[:].indirect(offsets[:, entries.start // 16 : entries.stop // 16])
 
-        nc.gpsimd.memset(x_plane[:].bitcast(I32), 0)
         make_identity(nc, ident[:])
 
         nc.sync.dma_start(new_col[:], new[0].rearrange("(p i) -> p i", i=PACK))
@@ -103,14 +102,14 @@ def tile_picked_wema_none_lo_kernel(
 
         halves = [first, second]
 
-        def buffer(tag, width=HALF):
-            return keep.tile([P, width], F32, name="buffer", tag=tag, align_bytes=64)
+        def buffer(tag, *shape):
+            return keep.tile([P, *shape], F32, name="buffer", tag=tag, align_bytes=64)
 
-        def project(t, entries, bank):
-            acc = psum.tile([P, entries.stop - entries.start], F32, name="acc", tag="bank_" + bank)
-            for h in range(entries.start // HALF, entries.stop // HALF):
+        def weigh_new(fresh, tiles, h, bank):
+            acc = psum.tile([P, len(tiles), HALF], F32, name="acc", tag="bank_" + bank)
+            for i, t in enumerate(tiles):
                 nc.tensor.matmul_mx(
-                    out=acc[:, h * HALF - entries.start : (h + 1) * HALF - entries.start],
+                    out=acc[:, i, :],
                     lhsT=stationary[t][0].bitcast(FP8X4),
                     lhsT_scale=stationary[t][1],
                     rhs=x_codes[h][:].bitcast(FP8X4),
@@ -118,38 +117,28 @@ def tile_picked_wema_none_lo_kernel(
                     start=True,
                     stop=True,
                 )
-            return acc
+            nc.vector.tensor_tensor(fresh, acc[:], new_row[:, halves[h]].unsqueeze(1).to_broadcast([P, len(tiles), HALF]), MULT)
 
-        def weigh(acc, entries, tag):
-            fresh = buffer(tag, entries.stop - entries.start)
-            nc.vector.tensor_tensor(fresh[:], acc, new_row[:, entries], MULT)
-            return fresh
-
-        def weigh_new(t, entries, bank, tag):
-            return weigh(project(t, entries, bank)[:], entries, tag)
-
-        def look_up(t, h, tag):
-            plain = buffer(tag)
+        def look_up(t, h, name):
+            plain = turns.tile([P, HALF], F32, name=name, offset=(2 * t + h) * HALF * 4, align_bytes=64)
             nc.scalar.activation(plain[:], listed(windows[t], halves[h]), COPY)
             return plain
 
         def weigh_old(plain, h, tag):
-            kept = buffer(tag)
+            kept = buffer(tag, HALF)
             nc.vector.tensor_tensor(kept[:], plain[:], old_row[:, halves[h]], MULT)
             return kept
 
-        def gather(t, entries, tag):
-            kept = buffer(tag, entries.stop - entries.start)
-            nc.vector.tensor_tensor(kept[:], listed(windows[t], entries), old_row[:, entries], MULT)
+        def gather(t, tag):
+            kept = buffer(tag, T)
+            nc.vector.tensor_tensor(kept[:], listed(windows[t], whole), old_row[:], MULT)
             return kept
 
-        def add_and_scatter(t, entries, kept, fresh, tag):
-            moved = buffer(tag, entries.stop - entries.start)
+        def add_and_scatter(t, h, kept, fresh):
+            moved = buffer("moved_%d%d" % (t, h), HALF)
             nc.vector.tensor_tensor(moved[:], kept, fresh, ADD)
-            nc.scalar.activation(listed(windows[t], entries), moved[:], COPY)
-
-        def scatter_sum(t, entries, kept, fresh):
-            nc.vector.tensor_tensor(listed(windows[t], entries), kept, fresh, ADD)
+            nc.scalar.activation(listed(windows[t], halves[h]), moved[:], COPY)
+            return moved
 
         def store(t):
             nc.sync.dma_start(out_rows[:, t, :], windows[t][:])
@@ -160,53 +149,48 @@ def tile_picked_wema_none_lo_kernel(
         plain_0b = look_up(0, 1, "plain_0b")
         plain_1a = look_up(1, 0, "plain_1a")
         plain_1b = look_up(1, 1, "plain_1b")
-        fresh_0a = weigh_new(0, first, "new", "fresh_0a")
+        fresh_a = buffer("old_col", 2, HALF)
+        weigh_new(fresh_a[:, 0:1, :], (0,), 0, "new")
+        weigh_new(fresh_a[:, 1:2, :], (1,), 0, "old")
         kept_0a = weigh_old(plain_0a, 0, "kept_0a")
-        fresh_1a = weigh_new(1, first, "old", "fresh_1a")
-        add_and_scatter(0, first, kept_0a[:], fresh_0a[:], "moved_0a")
-        kept_1a = weigh_old(plain_1a, 0, "kept_0a")
-        kept_0b = weigh_old(plain_0b, 1, "fresh_0a")
-        add_and_scatter(1, first, kept_1a[:], fresh_1a[:], "moved_1a")
-        fresh_0b = weigh_new(0, second, "new", "plain_1a")
-        kept_1b = weigh_old(plain_1b, 1, "plain_0b")
-        fresh_1b = weigh_new(1, second, "old", "fresh_1a")
-        add_and_scatter(0, second, kept_0b[:], fresh_0b[:], "moved_0b")
+        kept_0b = weigh_old(plain_0b, 1, "kept_0b")
+        moved_0a = add_and_scatter(0, 0, kept_0a[:], fresh_a[:, 0, :])
+        fresh_high = buffer("fresh_high", 2, T)
+        weigh_new(fresh_high[:, :, first], (2, 3), 0, "high")
+        kept_1a = weigh_old(plain_1a, 0, "kept_1a")
+        fresh_b = turns.tile([P, 2, HALF], F32, name="fresh_b", offset=0, align_bytes=64)
+        weigh_new(fresh_b[:], (0, 1), 1, "new")
+        moved_1a = add_and_scatter(1, 0, kept_1a[:], fresh_a[:, 1, :])
+        kept_2 = gather(2, "kept_1a")
+        moved_0b = add_and_scatter(0, 1, kept_0b[:], fresh_b[:, 0, :])
         store(0)
-        kept_2 = gather(2, whole, "plain_1b")
-        add_and_scatter(1, second, kept_1b[:], fresh_1b[:], "moved_1b")
+        weigh_new(fresh_high[:, :, second], (2, 3), 1, "old")
+        kept_1b = weigh_old(plain_1b, 1, "kept_1b")
+        moved_2a = add_and_scatter(2, 0, kept_2[:, first], fresh_high[:, 0, first])
+        kept_3 = gather(3, "kept_0b")
+        moved_1b = add_and_scatter(1, 1, kept_1b[:], fresh_b[:, 1, :])
         store(1)
-        scalar_part, vector_part = slice(0, SPLIT), slice(SPLIT, T)
-        acc_2 = project(2, whole, "two")
-        fresh_2 = weigh(acc_2[:, scalar_part], scalar_part, "fresh_0a")
-        kept_3 = gather(3, whole, "plain_1a")
-        fresh_3 = weigh_new(3, whole, "three", "plain_0b")
-        add_and_scatter(2, first, kept_2[:, first], fresh_2[:, first], "moved_2a")
-        scatter_sum(3, second, kept_3[:, second], fresh_3[:, second])
-        add_and_scatter(3, first, kept_3[:, first], fresh_3[:, first], "moved_3a")
+        moved_3 = buffer("moved_3", T)
+        nc.vector.tensor_tensor(moved_3[:], kept_3[:], fresh_high[:, 1, :], ADD)
+        moved_2b = add_and_scatter(2, 1, kept_2[:, second], fresh_high[:, 0, second])
+        nc.vector.tensor_copy(listed(windows[3], whole), moved_3[:])
         store(3)
-        fresh_2c = weigh(acc_2[:, vector_part], vector_part, "plain_1a")
-        scatter_sum(2, vector_part, kept_2[:, vector_part], fresh_2c[:])
-        ending = slice(HALF, SPLIT)
-        add_and_scatter(2, ending, kept_2[:, ending], fresh_2[:, ending], "plain_0b")
         store(2)
 
         spans = [slice(0, 384), slice(384, 640), slice(640, U)]
         sides = [slice(0, 640), slice(640, U)]
         pairs = [
-            keep.tile([P, 2, side.stop - side.start, 2], BF16, name="pairs", tag=tag, align_bytes=64)
-            for side, tag in zip(sides, ("plain_1b", "fresh_0a"))
+            keep.tile([P, 2, 640, 2], BF16, name="pairs", tag="kept_1a", align_bytes=64),
+            keep.tile([P, 2, U - 640, 2], BF16, name="pairs", tag="fresh_high", align_bytes=64),
         ]
         for t in range(2):
             for side, tile in zip(sides, pairs):
-                nc.vector.tensor_copy(out=tile[:, 0, :, t], in_=windows[t][:, side])
-        shared = sides[1].stop - sides[1].start
-        nc.vector.tensor_copy(
-            out=pairs[1][:, 1, :, :], in_=windows[3][:, sides[1]].unsqueeze(2).to_broadcast([P, shared, 2])
-        )
+                nc.gpsimd.tensor_scalar(tile[:, 0, :, t], windows[t][:, side], 1.0, -0.0, MULT, ADD)
         nc.vector.tensor_copy(out=pairs[0][:, 1, :, 1], in_=windows[3][:, sides[0]])
         for span in spans[:2]:
             nc.vector.tensor_copy(out=pairs[0][:, 1, span, 0], in_=windows[2][:, span])
-        nc.scalar.copy(out=pairs[1][:, 1, :, 0], in_=windows[2][:, sides[1]])
+        for t in (3, 2):
+            nc.scalar.copy(out=pairs[1][:, 1, :, t - 2], in_=windows[t][:, sides[1]])
 
         grouped = []
         for c, span in enumerate(spans):

@@ -7,6 +7,7 @@ K, T, N, U = 512, 512, 512, 1024
 P = 128
 PACK = 4
 HALF = T // 2
+SPLIT = 384
 FLOPS = 2 * K * N * T
 
 F32 = mybir.dt.float32
@@ -38,11 +39,11 @@ def tile_picked_wema_none_lo_kernel(
 
         offsets = keep.tile([P, T // 16], U16, name="offsets")
         windows = [keep.tile([P, U], F32, name="window%d" % t) for t in range(PACK)]
-        w_raw = [keep.tile([P, 2, N], F32, name="w_raw0"), turns.tile([P, 2, N], F32, name="w_raw1", offset=0, align_bytes=64)]
+        w_raw = [keep.tile([P, 2, N], F32, name="w_raw0"), turns.tile([P, 2, N], F32, name="w_raw1", offset=3 * HALF * 4, align_bytes=64)]
         x_codes = [keep.tile([P, HALF], I32, name="x_codes%d" % h, align_bytes=64) for h in range(2)]
         x_plane = keep.tile([P, T], U8, name="x_plane", align_bytes=64)
         ident = keep.tile([P, P], F32, name="ident")
-        old_col = keep.tile([P, PACK], F32, name="old_col", tag="old_col", align_bytes=64)
+        old_col = keep.tile([P, PACK], F32, name="old_col")
         new_col = keep.tile([P, PACK], F32, name="new_col")
 
         def listed(window, entries):
@@ -66,27 +67,26 @@ def tile_picked_wema_none_lo_kernel(
         for t in (2, 3):
             nc.sync.dma_start(windows[t][:], mem_rows[:, t, :])
 
-        def spread(column, name):
+        def spread(column, name, copy):
             turned = psum.tile([P, PACK, P], F32, name="turned", tag="bank_" + name)
             for i in range(PACK):
                 nc.tensor.transpose(turned[:, i, :], column[:, i : i + 1].to_broadcast([P, P]), ident[:])
             row = keep.tile([P, T], F32, name=name + "_row")
-            nc.scalar.activation(
-                row[:].rearrange("q (p i) -> q p i", i=PACK), turned[:].rearrange("q i p -> q p i"), COPY
-            )
-            return row
+            copy(row[:].rearrange("q (p i) -> q p i", i=PACK), turned[:].rearrange("q i p -> q p i"))
+            return row, turned
 
-        new_row = spread(new_col, "new")
-        old_row = spread(old_col, "old")
+        new_row, new_bank = spread(new_col, "new", lambda out, in_: nc.scalar.activation(out, in_, COPY))
+        old_row, old_bank = spread(old_col, "old", nc.vector.tensor_copy)
+        old_turned = old_bank[:].rearrange("q i p -> q p i")
 
         w_low = keep.tile([P, 2, P, PACK], BF16, name="w_low", align_bytes=64)
-        w_high = keep.tile([P, 2, P, PACK], BF16, name="w_high", tag="old_col", align_bytes=64)
+        w_high = keep.tile([P, 2, P, PACK], BF16, name="w_high", tag="w_high", align_bytes=64)
         for h in range(2):
             src = w_raw[h][:].rearrange("p j (m t) -> p m t j", t=PACK)
             nc.vector.tensor_copy(
                 out=w_low[:, :, :, 2 * h : 2 * h + 2].rearrange("p t m j -> p m t j"), in_=src[:, :, 0:2, :]
             )
-            nc.scalar.copy(
+            nc.vector.tensor_copy(
                 out=w_high[:, :, :, 2 * h : 2 * h + 2].rearrange("p t m j -> p m t j"), in_=src[:, :, 2:4, :]
             )
         stationary = []
@@ -120,13 +120,18 @@ def tile_picked_wema_none_lo_kernel(
             nc.vector.tensor_tensor(fresh, acc[:], new_row[:, halves[h]].unsqueeze(1).to_broadcast([P, len(tiles), HALF]), MULT)
 
         def look_up(t, h, name):
-            plain = turns.tile([P, HALF], F32, name=name, offset=(2 * t + h) * HALF * 4, align_bytes=64)
+            plain = turns.tile([P, HALF], F32, name=name, offset=(3 + (0, 3, 1, 2)[2 * t + h]) * HALF * 4, align_bytes=64)
             nc.scalar.activation(plain[:], listed(windows[t], halves[h]), COPY)
             return plain
 
         def weigh_old(plain, h, tag):
             kept = buffer(tag, HALF)
-            nc.vector.tensor_tensor(kept[:], plain[:], old_row[:, halves[h]], MULT)
+            nc.vector.tensor_tensor(
+                kept[:].rearrange("q (p i) -> q p i", i=PACK),
+                plain[:].rearrange("q (p i) -> q p i", i=PACK),
+                old_turned[:, h * HALF // PACK : (h + 1) * HALF // PACK, :],
+                MULT,
+            )
             return kept
 
         def gather(t, tag):
@@ -134,11 +139,13 @@ def tile_picked_wema_none_lo_kernel(
             nc.vector.tensor_tensor(kept[:], listed(windows[t], whole), old_row[:], MULT)
             return kept
 
-        def add_and_scatter(t, h, kept, fresh):
-            moved = buffer("moved_%d%d" % (t, h), HALF)
-            nc.vector.tensor_tensor(moved[:], kept, fresh, ADD)
-            nc.scalar.activation(listed(windows[t], halves[h]), moved[:], COPY)
+        def add(engine, kept, fresh, tag):
+            moved = buffer(tag, fresh.shape[1])
+            engine.tensor_tensor(moved[:], kept, fresh, ADD)
             return moved
+
+        def scatter(t, entries, moved):
+            nc.scalar.activation(listed(windows[t], entries), moved[:], COPY)
 
         def store(t):
             nc.sync.dma_start(out_rows[:, t, :], windows[t][:])
@@ -149,39 +156,45 @@ def tile_picked_wema_none_lo_kernel(
         plain_0b = look_up(0, 1, "plain_0b")
         plain_1a = look_up(1, 0, "plain_1a")
         plain_1b = look_up(1, 1, "plain_1b")
-        fresh_a = buffer("old_col", 2, HALF)
-        weigh_new(fresh_a[:, 0:1, :], (0,), 0, "new")
-        weigh_new(fresh_a[:, 1:2, :], (1,), 0, "old")
+        fresh_a = buffer("w_high", 2, HALF)
+        weigh_new(fresh_a[:, 0:1, :], (0,), 0, "one")
+        weigh_new(fresh_a[:, 1:2, :], (1,), 0, "new")
         kept_0a = weigh_old(plain_0a, 0, "kept_0a")
+        moved_0a = add(nc.gpsimd, kept_0a[:], fresh_a[:, 0, :], "moved_0a")
+        scatter(0, first, moved_0a)
         kept_0b = weigh_old(plain_0b, 1, "kept_0b")
-        moved_0a = add_and_scatter(0, 0, kept_0a[:], fresh_a[:, 0, :])
-        fresh_high = buffer("fresh_high", 2, T)
+        fresh_high = turns.tile([P, 2, T], F32, name="fresh_high", offset=0, align_bytes=64)
         weigh_new(fresh_high[:, :, first], (2, 3), 0, "high")
         kept_1a = weigh_old(plain_1a, 0, "kept_1a")
-        fresh_b = turns.tile([P, 2, HALF], F32, name="fresh_b", offset=0, align_bytes=64)
-        weigh_new(fresh_b[:], (0, 1), 1, "new")
-        moved_1a = add_and_scatter(1, 0, kept_1a[:], fresh_a[:, 1, :])
-        kept_2 = gather(2, "kept_1a")
-        moved_0b = add_and_scatter(0, 1, kept_0b[:], fresh_b[:, 0, :])
+        moved_1a = add(nc.gpsimd, kept_1a[:], fresh_a[:, 1, :], "moved_1a")
+        scatter(1, first, moved_1a)
+        fresh_b = turns.tile([P, 2, HALF], F32, name="fresh_b", offset=6 * HALF * 4, align_bytes=64)
+        weigh_new(fresh_b[:], (0, 1), 1, "one")
+        moved_0b = add(nc.gpsimd, kept_0b[:], fresh_b[:, 0, :], "moved_0b")
+        scatter(0, second, moved_0b)
         store(0)
-        weigh_new(fresh_high[:, :, second], (2, 3), 1, "old")
         kept_1b = weigh_old(plain_1b, 1, "kept_1b")
-        moved_2a = add_and_scatter(2, 0, kept_2[:, first], fresh_high[:, 0, first])
+        weigh_new(fresh_high[:, :, second], (2, 3), 1, "new")
+        kept_2 = gather(2, "kept_1a")
         kept_3 = gather(3, "kept_0b")
-        moved_1b = add_and_scatter(1, 1, kept_1b[:], fresh_b[:, 1, :])
+        scalar_part, vector_part = slice(0, SPLIT), slice(SPLIT, T)
+        moved_2c = add(nc.vector, kept_2[:, vector_part], fresh_high[:, 0, vector_part], "moved_2c")
+        moved_1b = add(nc.vector, kept_1b[:], fresh_b[:, 1, :], "moved_1b")
+        scatter(1, second, moved_1b)
         store(1)
-        moved_3 = buffer("moved_3", T)
-        nc.vector.tensor_tensor(moved_3[:], kept_3[:], fresh_high[:, 1, :], ADD)
-        moved_2b = add_and_scatter(2, 1, kept_2[:, second], fresh_high[:, 0, second])
+        moved_3 = add(nc.vector, kept_3[:], fresh_high[:, 1, :], "moved_3")
+        nc.vector.tensor_copy(listed(windows[2], vector_part), moved_2c[:])
         nc.vector.tensor_copy(listed(windows[3], whole), moved_3[:])
-        store(3)
+        moved_2 = add(nc.gpsimd, kept_2[:, scalar_part], fresh_high[:, 0, scalar_part], "kept_1b")
+        scatter(2, scalar_part, moved_2)
         store(2)
+        store(3)
 
         spans = [slice(0, 384), slice(384, 640), slice(640, U)]
         sides = [slice(0, 640), slice(640, U)]
         pairs = [
             keep.tile([P, 2, 640, 2], BF16, name="pairs", tag="kept_1a", align_bytes=64),
-            keep.tile([P, 2, U - 640, 2], BF16, name="pairs", tag="fresh_high", align_bytes=64),
+            turns.tile([P, 2, U - 640, 2], BF16, name="pairs_scalar", offset=0, align_bytes=64),
         ]
         for t in range(2):
             for side, tile in zip(sides, pairs):
@@ -189,7 +202,7 @@ def tile_picked_wema_none_lo_kernel(
         nc.vector.tensor_copy(out=pairs[0][:, 1, :, 1], in_=windows[3][:, sides[0]])
         for span in spans[:2]:
             nc.vector.tensor_copy(out=pairs[0][:, 1, span, 0], in_=windows[2][:, span])
-        for t in (3, 2):
+        for t in (2, 3):
             nc.scalar.copy(out=pairs[1][:, 1, :, t - 2], in_=windows[t][:, sides[1]])
 
         grouped = []

@@ -145,7 +145,7 @@ def tile_picked_wema_none_lo_kernel(
             return moved
 
         def scatter(t, entries, moved):
-            nc.scalar.activation(listed(windows[t], entries), moved[:], COPY)
+            nc.scalar.activation(listed(windows[t], entries), moved, COPY)
 
         def store(t):
             nc.sync.dma_start(out_rows[:, t, :], windows[t][:])
@@ -161,32 +161,31 @@ def tile_picked_wema_none_lo_kernel(
         weigh_new(fresh_a[:, 1:2, :], (1,), 0, "new")
         kept_0a = weigh_old(plain_0a, 0, "kept_0a")
         moved_0a = add(nc.gpsimd, kept_0a[:], fresh_a[:, 0, :], "moved_0a")
-        scatter(0, first, moved_0a)
+        scatter(0, first, moved_0a[:])
         kept_0b = weigh_old(plain_0b, 1, "kept_0b")
         fresh_high = turns.tile([P, 2, T], F32, name="fresh_high", offset=0, align_bytes=64)
         weigh_new(fresh_high[:, :, first], (2, 3), 0, "high")
         kept_1a = weigh_old(plain_1a, 0, "kept_1a")
         moved_1a = add(nc.gpsimd, kept_1a[:], fresh_a[:, 1, :], "moved_1a")
-        scatter(1, first, moved_1a)
+        scatter(1, first, moved_1a[:])
         fresh_b = turns.tile([P, 2, HALF], F32, name="fresh_b", offset=6 * HALF * 4, align_bytes=64)
         weigh_new(fresh_b[:], (0, 1), 1, "one")
         moved_0b = add(nc.gpsimd, kept_0b[:], fresh_b[:, 0, :], "moved_0b")
-        scatter(0, second, moved_0b)
+        scatter(0, second, moved_0b[:])
         store(0)
         kept_1b = weigh_old(plain_1b, 1, "kept_1b")
         weigh_new(fresh_high[:, :, second], (2, 3), 1, "new")
         kept_2 = gather(2, "kept_1a")
         kept_3 = gather(3, "kept_0b")
         scalar_part, vector_part = slice(0, SPLIT), slice(SPLIT, T)
-        moved_2c = add(nc.vector, kept_2[:, vector_part], fresh_high[:, 0, vector_part], "moved_2c")
         moved_1b = add(nc.vector, kept_1b[:], fresh_b[:, 1, :], "moved_1b")
-        scatter(1, second, moved_1b)
+        scatter(1, second, moved_1b[:])
         store(1)
+        moved_2 = add(nc.vector, kept_2[:], fresh_high[:, 0, :], "moved_2")
         moved_3 = add(nc.vector, kept_3[:], fresh_high[:, 1, :], "moved_3")
-        nc.vector.tensor_copy(listed(windows[2], vector_part), moved_2c[:])
+        nc.vector.tensor_copy(listed(windows[2], vector_part), moved_2[:, vector_part])
+        scatter(2, scalar_part, moved_2[:, scalar_part])
         nc.vector.tensor_copy(listed(windows[3], whole), moved_3[:])
-        moved_2 = add(nc.gpsimd, kept_2[:, scalar_part], fresh_high[:, 0, scalar_part], "kept_1b")
-        scatter(2, scalar_part, moved_2)
         store(2)
         store(3)
 

@@ -39,20 +39,20 @@ def tile_picked_wema_none_lo_kernel(
 
         offsets = keep.tile([P, T // 16], U16, name="offsets")
         windows = [keep.tile([P, U], F32, name="window%d" % t) for t in range(PACK)]
-        w_raw = [keep.tile([P, 2, N], F32, name="w_raw0"), turns.tile([P, 2, N], F32, name="w_raw1", offset=3 * HALF * 4, align_bytes=64)]
-        x_codes = [keep.tile([P, HALF], I32, name="x_codes%d" % h, align_bytes=64) for h in range(2)]
+        w_raw = [keep.tile([P, 2, N], F32, name="w_raw%d" % h) for h in range(2)]
+        x_codes = [turns.tile([P, HALF], I32, name="x_codes%d" % h, offset=(27, 40)[h] * HALF * 2, align_bytes=64) for h in range(2)]
         x_plane = keep.tile([P, T], U8, name="x_plane", align_bytes=64)
         ident = keep.tile([P, P], F32, name="ident")
         old_col = keep.tile([P, PACK], F32, name="old_col")
-        new_col = keep.tile([P, PACK], F32, name="new_col")
+        new_col = turns.tile([P, 3 * HALF], F32, name="new_col", offset=HALF * 4, align_bytes=64)
 
         def listed(window, entries):
             return window[:].indirect(offsets[:, entries.start // 16 : entries.stop // 16])
 
         make_identity(nc, ident[:])
 
-        nc.sync.dma_start(new_col[:], new[0].rearrange("(p i) -> p i", i=PACK))
         nc.sync.dma_start(old_col[:], old[0].rearrange("(p i) -> p i", i=PACK))
+        nc.sync.dma_start(new_col[:, :PACK], new[0].rearrange("(p i) -> p i", i=PACK))
         nc.sync.dma_start(offsets[:], slot)
         for h in range(2):
             nc.sync.dma_start(w_raw[h][:], w_rows[:, 2 * h : 2 * h + 2, :])
@@ -67,20 +67,22 @@ def tile_picked_wema_none_lo_kernel(
         for t in (2, 3):
             nc.sync.dma_start(windows[t][:], mem_rows[:, t, :])
 
-        def spread(column, name, copy):
+        def spread(column, name):
             turned = psum.tile([P, PACK, P], F32, name="turned", tag="bank_" + name)
             for i in range(PACK):
                 nc.tensor.transpose(turned[:, i, :], column[:, i : i + 1].to_broadcast([P, P]), ident[:])
             row = keep.tile([P, T], F32, name=name + "_row")
-            copy(row[:].rearrange("q (p i) -> q p i", i=PACK), turned[:].rearrange("q i p -> q p i"))
+            nc.scalar.activation(
+                row[:].rearrange("q (p i) -> q p i", i=PACK), turned[:].rearrange("q i p -> q p i"), COPY
+            )
             return row, turned
 
-        new_row, new_bank = spread(new_col, "new", lambda out, in_: nc.scalar.activation(out, in_, COPY))
-        old_row, old_bank = spread(old_col, "old", nc.vector.tensor_copy)
+        old_row, old_bank = spread(old_col, "old")
+        new_row, new_bank = spread(new_col, "new")
         old_turned = old_bank[:].rearrange("q i p -> q p i")
 
-        w_low = keep.tile([P, 2, P, PACK], BF16, name="w_low", align_bytes=64)
-        w_high = keep.tile([P, 2, P, PACK], BF16, name="w_high", tag="w_high", align_bytes=64)
+        w_low = turns.tile([P, 2, P, PACK], BF16, name="w_low", offset=4 * HALF * 4, align_bytes=64)
+        w_high = turns.tile([P, 2, P, PACK], BF16, name="w_high", offset=6 * HALF * 4, align_bytes=64)
         for h in range(2):
             src = w_raw[h][:].rearrange("p j (m t) -> p m t j", t=PACK)
             nc.vector.tensor_copy(
@@ -120,12 +122,15 @@ def tile_picked_wema_none_lo_kernel(
             nc.vector.tensor_tensor(fresh, acc[:], new_row[:, halves[h]].unsqueeze(1).to_broadcast([P, len(tiles), HALF]), MULT)
 
         def look_up(t, h, name):
-            plain = turns.tile([P, HALF], F32, name=name, offset=(3 + (0, 3, 1, 2)[2 * t + h]) * HALF * 4, align_bytes=64)
+            plain = turns.tile([P, HALF], F32, name=name, offset=(2 * t + h) * HALF * 4, align_bytes=64)
             nc.scalar.activation(plain[:], listed(windows[t], halves[h]), COPY)
             return plain
 
-        def weigh_old(plain, h, tag):
-            kept = buffer(tag, HALF)
+        def placed(name, place, *shape):
+            return turns.tile([P, *shape], F32, name=name, offset=place * HALF * 4, align_bytes=64)
+
+        def weigh_old(plain, h, name, place):
+            kept = placed(name, place, HALF)
             nc.vector.tensor_tensor(
                 kept[:].rearrange("q (p i) -> q p i", i=PACK),
                 plain[:].rearrange("q (p i) -> q p i", i=PACK),
@@ -134,8 +139,8 @@ def tile_picked_wema_none_lo_kernel(
             )
             return kept
 
-        def gather(t, tag):
-            kept = buffer(tag, T)
+        def gather(t, place):
+            kept = placed("kept_%d" % t, place, T)
             nc.vector.tensor_tensor(kept[:], listed(windows[t], whole), old_row[:], MULT)
             return kept
 
@@ -152,31 +157,31 @@ def tile_picked_wema_none_lo_kernel(
 
         whole = slice(0, T)
 
-        plain_0a = look_up(0, 0, "plain_0a")
         plain_0b = look_up(0, 1, "plain_0b")
         plain_1a = look_up(1, 0, "plain_1a")
         plain_1b = look_up(1, 1, "plain_1b")
-        fresh_a = buffer("w_high", 2, HALF)
+        fresh_a = turns.tile([P, 2, HALF], F32, name="fresh_a", offset=6 * HALF * 4, align_bytes=64)
+        kept_0a = turns.tile([P, HALF], F32, name="kept_0a", offset=4 * HALF * 4, align_bytes=64)
+        nc.vector.tensor_tensor(kept_0a[:], listed(windows[0], first), old_row[:, first], MULT)
         weigh_new(fresh_a[:, 0:1, :], (0,), 0, "one")
         weigh_new(fresh_a[:, 1:2, :], (1,), 0, "new")
-        kept_0a = weigh_old(plain_0a, 0, "kept_0a")
         moved_0a = add(nc.gpsimd, kept_0a[:], fresh_a[:, 0, :], "moved_0a")
         scatter(0, first, moved_0a[:])
-        kept_0b = weigh_old(plain_0b, 1, "kept_0b")
-        fresh_high = turns.tile([P, 2, T], F32, name="fresh_high", offset=0, align_bytes=64)
+        fresh_high = turns.tile([P, 2, T], F32, name="fresh_high", offset=8 * HALF * 4, align_bytes=64)
         weigh_new(fresh_high[:, :, first], (2, 3), 0, "high")
-        kept_1a = weigh_old(plain_1a, 0, "kept_1a")
+        kept_0b = weigh_old(plain_0b, 1, "kept_0b", 13)
+        kept_1a = weigh_old(plain_1a, 0, "kept_1a", 14)
         moved_1a = add(nc.gpsimd, kept_1a[:], fresh_a[:, 1, :], "moved_1a")
         scatter(1, first, moved_1a[:])
-        fresh_b = turns.tile([P, 2, HALF], F32, name="fresh_b", offset=6 * HALF * 4, align_bytes=64)
+        fresh_b = turns.tile([P, 2, HALF], F32, name="fresh_b", offset=0, align_bytes=64)
         weigh_new(fresh_b[:], (0, 1), 1, "one")
         moved_0b = add(nc.gpsimd, kept_0b[:], fresh_b[:, 0, :], "moved_0b")
         scatter(0, second, moved_0b[:])
         store(0)
-        kept_1b = weigh_old(plain_1b, 1, "kept_1b")
+        kept_1b = weigh_old(plain_1b, 1, "kept_1b", 20)
         weigh_new(fresh_high[:, :, second], (2, 3), 1, "new")
-        kept_2 = gather(2, "kept_1a")
-        kept_3 = gather(3, "kept_0b")
+        kept_2 = gather(2, 14)
+        kept_3 = gather(3, 12)
         scalar_part, vector_part = slice(0, SPLIT), slice(SPLIT, T)
         moved_1b = add(nc.vector, kept_1b[:], fresh_b[:, 1, :], "moved_1b")
         scatter(1, second, moved_1b[:])
@@ -192,8 +197,8 @@ def tile_picked_wema_none_lo_kernel(
         spans = [slice(0, 384), slice(384, 640), slice(640, U)]
         sides = [slice(0, 640), slice(640, U)]
         pairs = [
-            keep.tile([P, 2, 640, 2], BF16, name="pairs", tag="kept_1a", align_bytes=64),
-            turns.tile([P, 2, U - 640, 2], BF16, name="pairs_scalar", offset=0, align_bytes=64),
+            turns.tile([P, 2, 640, 2], BF16, name="pairs", offset=14 * HALF * 4, align_bytes=64),
+            turns.tile([P, 2, U - 640, 2], BF16, name="pairs_scalar", offset=8 * HALF * 4, align_bytes=64),
         ]
         for t in range(2):
             for side, tile in zip(sides, pairs):

@@ -8,6 +8,7 @@ P = 128
 PACK = 4
 HALF = T // 2
 SPLIT = 384
+SIDE = 608
 FLOPS = 2 * K * N * T
 
 F32 = mybir.dt.float32
@@ -165,11 +166,12 @@ def tile_picked_wema_none_lo_kernel(
         nc.vector.tensor_tensor(kept_0a[:], listed(windows[0], first), old_row[:, first], MULT)
         weigh_new(fresh_a[:, 0:1, :], (0,), 0, "one")
         weigh_new(fresh_a[:, 1:2, :], (1,), 0, "new")
+        kept_0b = placed("kept_0b", 12, HALF)
+        nc.gpsimd.tensor_tensor(kept_0b[:], plain_0b[:], old_row[:, second], MULT)
         moved_0a = add(nc.gpsimd, kept_0a[:], fresh_a[:, 0, :], "moved_0a")
         scatter(0, first, moved_0a[:])
         fresh_high = turns.tile([P, 2, T], F32, name="fresh_high", offset=8 * HALF * 4, align_bytes=64)
         weigh_new(fresh_high[:, :, first], (2, 3), 0, "high")
-        kept_0b = weigh_old(plain_0b, 1, "kept_0b", 13)
         kept_1a = weigh_old(plain_1a, 0, "kept_1a", 14)
         moved_1a = add(nc.gpsimd, kept_1a[:], fresh_a[:, 1, :], "moved_1a")
         scatter(1, first, moved_1a[:])
@@ -194,32 +196,33 @@ def tile_picked_wema_none_lo_kernel(
         store(2)
         store(3)
 
-        spans = [slice(0, 384), slice(384, 640), slice(640, U)]
-        sides = [slice(0, 640), slice(640, U)]
+        sides = [slice(0, SIDE), slice(SIDE, U)]
+        pieces = [(slice(0, 384), slice(384, SIDE)), (slice(0, 768 - SIDE), slice(768 - SIDE, U - SIDE))]
         pairs = [
-            turns.tile([P, 2, 640, 2], BF16, name="pairs", offset=14 * HALF * 4, align_bytes=64),
-            turns.tile([P, 2, U - 640, 2], BF16, name="pairs_scalar", offset=8 * HALF * 4, align_bytes=64),
+            turns.tile([P, 2, SIDE, 2], BF16, name="pairs", offset=14 * HALF * 4, align_bytes=64),
+            turns.tile([P, 2, U - SIDE, 2], BF16, name="pairs_scalar", offset=8 * HALF * 4, align_bytes=64),
         ]
         for t in range(2):
             for side, tile in zip(sides, pairs):
                 nc.gpsimd.tensor_scalar(tile[:, 0, :, t], windows[t][:, side], 1.0, -0.0, MULT, ADD)
-        nc.vector.tensor_copy(out=pairs[0][:, 1, :, 1], in_=windows[3][:, sides[0]])
-        for span in spans[:2]:
-            nc.vector.tensor_copy(out=pairs[0][:, 1, span, 0], in_=windows[2][:, span])
-        for t in (2, 3):
-            nc.scalar.copy(out=pairs[1][:, 1, :, t - 2], in_=windows[t][:, sides[1]])
 
-        grouped = []
-        for c, span in enumerate(spans):
-            tile = keep.tile([P, span.stop - span.start, PACK], BF16, name="grouped%d" % c, align_bytes=64)
-            word = I32 if c < 2 else U32
-            dst = tile[:].rearrange("p c t -> p (c t)").bitcast(word).rearrange("p (c h) -> p c h", h=2)
-            src = pairs[c // 2][:].rearrange("p h c e -> p h (c e)").bitcast(word).rearrange("p h c -> p c h")
-            if c < 2:
-                nc.vector.tensor_copy(out=dst, in_=src[:, span, :])
-            else:
-                nc.scalar.copy(out=dst, in_=src)
-            grouped.append(tile)
+        spans = [slice(0, 384), slice(384, 768), slice(768, U)]
+        grouped = [
+            keep.tile([P, span.stop - span.start, PACK], BF16, name="grouped%d" % c, align_bytes=64)
+            for c, span in enumerate(spans)
+        ]
+        targets = [
+            (grouped[0][:], grouped[1][:, : SIDE - 384, :]),
+            (grouped[1][:, SIDE - 384 :, :], grouped[2][:]),
+        ]
+        for e, (copy, word) in enumerate(((nc.vector.tensor_copy, I32), (nc.scalar.copy, U32))):
+            copy(out=pairs[e][:, 1, :, 1], in_=windows[3][:, sides[e]])
+            for piece in pieces[e]:
+                copy(out=pairs[e][:, 1, piece, 0], in_=windows[2][:, sides[e]][:, piece])
+            src = pairs[e][:].rearrange("p h c e -> p h (c e)").bitcast(word).rearrange("p h c -> p c h")
+            for piece, target in zip(pieces[e], targets[e]):
+                dst = target.rearrange("p c t -> p (c t)").bitcast(word).rearrange("p (c h) -> p c h", h=2)
+                copy(out=dst, in_=src[:, piece, :])
 
         y_plane = keep.tile([P, U], U8, name="y_plane", align_bytes=64)
         y_codes = keep.tile([P, U], I32, name="y_codes", align_bytes=64)

@@ -8,7 +8,8 @@ P = 128
 PACK = 4
 HALF = T // 2
 SPLIT = 384
-SIDE = 608
+EARLY = 320
+SIDE = 560
 FLOPS = 2 * K * N * T
 
 F32 = mybir.dt.float32
@@ -68,18 +69,19 @@ def tile_picked_wema_none_lo_kernel(
         for t in (2, 3):
             nc.sync.dma_start(windows[t][:], mem_rows[:, t, :])
 
-        def spread(column, name):
+        def spread(column, name, row):
             turned = psum.tile([P, PACK, P], F32, name="turned", tag="bank_" + name)
             for i in range(PACK):
                 nc.tensor.transpose(turned[:, i, :], column[:, i : i + 1].to_broadcast([P, P]), ident[:])
-            row = keep.tile([P, T], F32, name=name + "_row")
             nc.scalar.activation(
                 row[:].rearrange("q (p i) -> q p i", i=PACK), turned[:].rearrange("q i p -> q p i"), COPY
             )
-            return row, turned
+            return turned
 
-        old_row, old_bank = spread(old_col, "old")
-        new_row, new_bank = spread(new_col, "new")
+        old_row = turns.tile([P, T], F32, name="old_row", offset=32 * HALF * 4, align_bytes=64)
+        new_row = keep.tile([P, T], F32, name="new_row")
+        old_bank = spread(old_col, "old", old_row)
+        spread(new_col, "new", new_row)
         old_turned = old_bank[:].rearrange("q i p -> q p i")
 
         w_low = turns.tile([P, 2, P, PACK], BF16, name="w_low", offset=4 * HALF * 4, align_bytes=64)
@@ -140,9 +142,9 @@ def tile_picked_wema_none_lo_kernel(
             )
             return kept
 
-        def gather(t, place):
-            kept = placed("kept_%d" % t, place, T)
-            nc.vector.tensor_tensor(kept[:], listed(windows[t], whole), old_row[:], MULT)
+        def gather(t, entries, place):
+            kept = placed("kept_%d" % t, place, entries.stop - entries.start)
+            nc.vector.tensor_tensor(kept[:], listed(windows[t], entries), old_row[:, entries], MULT)
             return kept
 
         def add(engine, kept, fresh, tag):
@@ -158,7 +160,10 @@ def tile_picked_wema_none_lo_kernel(
 
         whole = slice(0, T)
 
-        plain_0b = look_up(0, 1, "plain_0b")
+        quarters = [slice(HALF + i * P, HALF + (i + 1) * P) for i in range(2)]
+        plain_0b = placed("plain_0b", 1, 2, P)
+        for i, quarter in enumerate(quarters):
+            nc.scalar.activation(plain_0b[:, i, :], listed(windows[0], quarter), COPY)
         plain_1a = look_up(1, 0, "plain_1a")
         plain_1b = look_up(1, 1, "plain_1b")
         fresh_a = turns.tile([P, 2, HALF], F32, name="fresh_a", offset=6 * HALF * 4, align_bytes=64)
@@ -167,10 +172,11 @@ def tile_picked_wema_none_lo_kernel(
         weigh_new(fresh_a[:, 0:1, :], (0,), 0, "one")
         weigh_new(fresh_a[:, 1:2, :], (1,), 0, "new")
         kept_0b = placed("kept_0b", 12, HALF)
-        nc.gpsimd.tensor_tensor(kept_0b[:], plain_0b[:], old_row[:, second], MULT)
+        for i, quarter in enumerate(quarters):
+            nc.gpsimd.tensor_tensor(kept_0b[:, i * P : (i + 1) * P], plain_0b[:, i, :], old_row[:, quarter], MULT)
         moved_0a = add(nc.gpsimd, kept_0a[:], fresh_a[:, 0, :], "moved_0a")
         scatter(0, first, moved_0a[:])
-        fresh_high = turns.tile([P, 2, T], F32, name="fresh_high", offset=8 * HALF * 4, align_bytes=64)
+        fresh_high = turns.tile([P, 2, T], F32, name="fresh_high", offset=24 * HALF * 4, align_bytes=64)
         weigh_new(fresh_high[:, :, first], (2, 3), 0, "high")
         kept_1a = weigh_old(plain_1a, 0, "kept_1a", 14)
         moved_1a = add(nc.gpsimd, kept_1a[:], fresh_a[:, 1, :], "moved_1a")
@@ -182,13 +188,17 @@ def tile_picked_wema_none_lo_kernel(
         store(0)
         kept_1b = weigh_old(plain_1b, 1, "kept_1b", 20)
         weigh_new(fresh_high[:, :, second], (2, 3), 1, "new")
-        kept_2 = gather(2, 14)
-        kept_3 = gather(3, 12)
-        scalar_part, vector_part = slice(0, SPLIT), slice(SPLIT, T)
+        early, late = slice(0, EARLY), slice(EARLY, T)
+        scalar_part, vector_part = slice(T - SPLIT, T), slice(0, T - SPLIT)
+        kept_2 = gather(2, early, 14)
+        kept_3 = gather(3, whole, 12)
+        moved_2 = buffer("moved_2", T)
+        nc.vector.tensor_tensor(moved_2[:, early], kept_2[:], fresh_high[:, 0, early], ADD)
         moved_1b = add(nc.vector, kept_1b[:], fresh_b[:, 1, :], "moved_1b")
         scatter(1, second, moved_1b[:])
         store(1)
-        moved_2 = add(nc.vector, kept_2[:], fresh_high[:, 0, :], "moved_2")
+        kept_late = gather(2, late, 14)
+        nc.gpsimd.tensor_tensor(moved_2[:, late], kept_late[:], fresh_high[:, 0, late], ADD)
         moved_3 = add(nc.vector, kept_3[:], fresh_high[:, 1, :], "moved_3")
         nc.vector.tensor_copy(listed(windows[2], vector_part), moved_2[:, vector_part])
         scatter(2, scalar_part, moved_2[:, scalar_part])
@@ -198,13 +208,10 @@ def tile_picked_wema_none_lo_kernel(
 
         sides = [slice(0, SIDE), slice(SIDE, U)]
         pieces = [(slice(0, 384), slice(384, SIDE)), (slice(0, 768 - SIDE), slice(768 - SIDE, U - SIDE))]
-        pairs = [
-            turns.tile([P, 2, SIDE, 2], BF16, name="pairs", offset=14 * HALF * 4, align_bytes=64),
-            turns.tile([P, 2, U - SIDE, 2], BF16, name="pairs_scalar", offset=8 * HALF * 4, align_bytes=64),
-        ]
+        both = turns.tile([P, 2, U, 2], BF16, name="pairs", offset=32 * HALF * 4, align_bytes=64)
         for t in range(2):
-            for side, tile in zip(sides, pairs):
-                nc.gpsimd.tensor_scalar(tile[:, 0, :, t], windows[t][:, side], 1.0, -0.0, MULT, ADD)
+            nc.gpsimd.tensor_scalar(both[:, 0, :, t], windows[t][:], 1.0, -0.0, MULT, ADD)
+        pairs = [both[:, :, side, :] for side in sides]
 
         spans = [slice(0, 384), slice(384, 768), slice(768, U)]
         grouped = [
@@ -219,7 +226,7 @@ def tile_picked_wema_none_lo_kernel(
             copy(out=pairs[e][:, 1, :, 1], in_=windows[3][:, sides[e]])
             for piece in pieces[e]:
                 copy(out=pairs[e][:, 1, piece, 0], in_=windows[2][:, sides[e]][:, piece])
-            src = pairs[e][:].rearrange("p h c e -> p h (c e)").bitcast(word).rearrange("p h c -> p c h")
+            src = pairs[e].rearrange("p h c e -> p h (c e)").bitcast(word).rearrange("p h c -> p c h")
             for piece, target in zip(pieces[e], targets[e]):
                 dst = target.rearrange("p c t -> p (c t)").bitcast(word).rearrange("p (c h) -> p c h", h=2)
                 copy(out=dst, in_=src[:, piece, :])

from contextlib import ExitStack

import concourse.mybir as mybir
from concourse.masks import make_identity

K, T, N, U = 512, 512, 512, 1024
P = 128
PACK = 4
HALF = T // 2
SPLIT = 384
EARLY = 320
SIDE = 560
FLOPS = 2 * K * N * T

F32 = mybir.dt.float32
BF16 = mybir.dt.bfloat16
I32 = mybir.dt.int32
U32 = mybir.dt.uint32
U16 = mybir.dt.uint16
U8 = mybir.dt.uint8
FP8X4 = mybir.dt.float8_e4m3fn_x4
MULT = mybir.AluOpType.mult
ADD = mybir.AluOpType.add
COPY = mybir.ActivationFunctionType.Copy


def tile_picked_wema_none_lo_kernel(
    tc, x_words, x_scales, mem, w1, old, new, slot, out_0, out_1, out_2
):
    nc = tc.nc
    mem_rows = mem.rearrange("(p t) u -> p t u", t=PACK)
    out_rows = out_0.rearrange("(p t) u -> p t u", t=PACK)
    w_rows = w1.rearrange("(p j) c -> p j c", j=PACK)
    x_flat = x_words[0].rearrange("p n t -> p (n t)").bitcast(I32)
    first, second = slice(0, HALF), slice(HALF, T)

    with ExitStack() as ctx:
        keep = ctx.enter_context(tc.tile_pool(name="keep", bufs=1))
        turns = ctx.enter_context(tc.tile_pool(name="turns", bufs=1))
        psum = ctx.enter_context(tc.psum_pool(name="psum", bufs=1))

        offsets = keep.tile([P, T // 16], U16, name="offsets")
        windows = [keep.tile([P, U], F32, name="window%d" % t) for t in range(PACK)]
        w_raw = [keep.tile([P, 2, N], F32, name="w_raw%d" % h) for h in range(2)]
        x_codes = [turns.tile([P, HALF], I32, name="x_codes%d" % h, offset=(27, 40)[h] * HALF * 2, align_bytes=64) for h in range(2)]
        x_plane = keep.tile([P, T], U8, name="x_plane", align_bytes=64)
        ident = keep.tile([P, P], F32, name="ident")
        old_col = keep.tile([P, PACK], F32, name="old_col")
        new_col = turns.tile([P, 3 * HALF], F32, name="new_col", offset=HALF * 4, align_bytes=64)

        def listed(window, entries):
            return window[:].indirect(offsets[:, entries.start // 16 : entries.stop // 16])

        make_identity(nc, ident[:])

        nc.sync.dma_start(old_col[:], old[0].rearrange("(p i) -> p i", i=PACK))
        nc.sync.dma_start(new_col[:, :PACK], new[0].rearrange("(p i) -> p i", i=PACK))
        nc.sync.dma_start(offsets[:], slot)
        for h in range(2):
            nc.sync.dma_start(w_raw[h][:], w_rows[:, 2 * h : 2 * h + 2, :])
        for q in range(4):
            nc.sync.dma_start(
                x_plane[32 * q : 32 * q + 4, :].bitcast(I32), x_scales[0, 4 * q : 4 * q + 4, :].bitcast(I32)
            )
        nc.sync.dma_start(x_codes[0][:], x_flat[:, first])
        nc.sync.dma_start(windows[0][:], mem_rows[:, 0, :])
        nc.sync.dma_start(windows[1][:], mem_rows[:, 1, :])
        nc.sync.dma_start(x_codes[1][:], x_flat[:, second])
        for t in (2, 3):
            nc.sync.dma_start(windows[t][:], mem_rows[:, t, :])

        def spread(column, name, row):
            turned = psum.tile([P, PACK, P], F32, name="turned", tag="bank_" + name)
            for i in range(PACK):
                nc.tensor.transpose(turned[:, i, :], column[:, i : i + 1].to_broadcast([P, P]), ident[:])
            nc.scalar.activation(
                row[:].rearrange("q (p i) -> q p i", i=PACK), turned[:].rearrange("q i p -> q p i"), COPY
            )
            return turned

        old_row = turns.tile([P, T], F32, name="old_row", offset=32 * HALF * 4, align_bytes=64)
        new_row = keep.tile([P, T], F32, name="new_row")
        old_bank = spread(old_col, "old", old_row)
        spread(new_col, "new", new_row)
        old_turned = old_bank[:].rearrange("q i p -> q p i")

        w_low = turns.tile([P, 2, P, PACK], BF16, name="w_low", offset=4 * HALF * 4, align_bytes=64)
        w_high = turns.tile([P, 2, P, PACK], BF16, name="w_high", offset=6 * HALF * 4, align_bytes=64)
        for h in range(2):
            src = w_raw[h][:].rearrange("p j (m t) -> p m t j", t=PACK)
            nc.vector.tensor_copy(
                out=w_low[:, :, :, 2 * h : 2 * h + 2].rearrange("p t m j -> p m t j"), in_=src[:, :, 0:2, :]
            )
            nc.vector.tensor_copy(
                out=w_high[:, :, :, 2 * h : 2 * h + 2].rearrange("p t m j -> p m t j"), in_=src[:, :, 2:4, :]
            )
        stationary = []
        for grouped_w in (w_low[:, 0:1], w_low[:, 1:2], w_high[:]):
            width = grouped_w.shape[1] * P
            codes = keep.tile([P, width], U32, name="w_codes%d" % len(stationary), align_bytes=64)
            plane = keep.tile([P, width], U8, name="w_plane%d" % len(stationary), align_bytes=64)
            nc.vector.quantize_mx(
                out=codes[:].bitcast(FP8X4), scales=plane[:], in_=grouped_w.rearrange("p t m j -> p (t m j)")
            )
            for i in range(0, width, P):
                stationary.append((codes[:, i : i + P], plane[:, i : i + P]))

        halves = [first, second]

        def buffer(tag, *shape):
            return keep.tile([P, *shape], F32, name="buffer", tag=tag, align_bytes=64)

        def weigh_new(fresh, tiles, h, bank):
            acc = psum.tile([P, len(tiles), HALF], F32, name="acc", tag="bank_" + bank)
            for i, t in enumerate(tiles):
                nc.tensor.matmul_mx(
                    out=acc[:, i, :],
                    lhsT=stationary[t][0].bitcast(FP8X4),
                    lhsT_scale=stationary[t][1],
                    rhs=x_codes[h][:].bitcast(FP8X4),
                    rhs_scale=x_plane[:, halves[h]],
                    start=True,
                    stop=True,
                )
            nc.vector.tensor_tensor(fresh, acc[:], new_row[:, halves[h]].unsqueeze(1).to_broadcast([P, len(tiles), HALF]), MULT)

        def look_up(t, h, name):
            plain = turns.tile([P, HALF], F32, name=name, offset=(2 * t + h) * HALF * 4, align_bytes=64)
            nc.scalar.activation(plain[:], listed(windows[t], halves[h]), COPY)
            return plain

        def placed(name, place, *shape):
            return turns.tile([P, *shape], F32, name=name, offset=place * HALF * 4, align_bytes=64)

        def weigh_old(plain, h, name, place):
            kept = placed(name, place, HALF)
            nc.vector.tensor_tensor(
                kept[:].rearrange("q (p i) -> q p i", i=PACK),
                plain[:].rearrange("q (p i) -> q p i", i=PACK),
                old_turned[:, h * HALF // PACK : (h + 1) * HALF // PACK, :],
                MULT,
            )
            return kept

        def gather(t, entries, place):
            kept = placed("kept_%d" % t, place, entries.stop - entries.start)
            nc.vector.tensor_tensor(kept[:], listed(windows[t], entries), old_row[:, entries], MULT)
            return kept

        def add(engine, kept, fresh, tag):
            moved = buffer(tag, fresh.shape[1])
            engine.tensor_tensor(moved[:], kept, fresh, ADD)
            return moved

        def scatter(t, entries, moved):
            nc.scalar.activation(listed(windows[t], entries), moved, COPY)

        def store(t):
            nc.sync.dma_start(out_rows[:, t, :], windows[t][:])

        whole = slice(0, T)

        quarters = [slice(HALF + i * P, HALF + (i + 1) * P) for i in range(2)]
        plain_0b = placed("plain_0b", 1, 2, P)
        for i, quarter in enumerate(quarters):
            nc.scalar.activation(plain_0b[:, i, :], listed(windows[0], quarter), COPY)
        plain_1a = look_up(1, 0, "plain_1a")
        plain_1b = look_up(1, 1, "plain_1b")
        fresh_a = turns.tile([P, 2, HALF], F32, name="fresh_a", offset=6 * HALF * 4, align_bytes=64)
        kept_0a = turns.tile([P, HALF], F32, name="kept_0a", offset=4 * HALF * 4, align_bytes=64)
        nc.vector.tensor_tensor(kept_0a[:], listed(windows[0], first), old_row[:, first], MULT)
        weigh_new(fresh_a[:, 0:1, :], (0,), 0, "one")
        weigh_new(fresh_a[:, 1:2, :], (1,), 0, "new")
        kept_0b = placed("kept_0b", 12, HALF)
        for i, quarter in enumerate(quarters):
            nc.gpsimd.tensor_tensor(kept_0b[:, i * P : (i + 1) * P], plain_0b[:, i, :], old_row[:, quarter], MULT)
        moved_0a = add(nc.gpsimd, kept_0a[:], fresh_a[:, 0, :], "moved_0a")
        scatter(0, first, moved_0a[:])
        fresh_high = turns.tile([P, 2, T], F32, name="fresh_high", offset=24 * HALF * 4, align_bytes=64)
        weigh_new(fresh_high[:, :, first], (2, 3), 0, "high")
        kept_1a = weigh_old(plain_1a, 0, "kept_1a", 14)
        moved_1a = add(nc.gpsimd, kept_1a[:], fresh_a[:, 1, :], "moved_1a")
        scatter(1, first, moved_1a[:])
        fresh_b = turns.tile([P, 2, HALF], F32, name="fresh_b", offset=0, align_bytes=64)
        weigh_new(fresh_b[:], (0, 1), 1, "one")
        moved_0b = add(nc.gpsimd, kept_0b[:], fresh_b[:, 0, :], "moved_0b")
        scatter(0, second, moved_0b[:])
        store(0)
        kept_1b = weigh_old(plain_1b, 1, "kept_1b", 20)
        weigh_new(fresh_high[:, :, second], (2, 3), 1, "new")
        early, late = slice(0, EARLY), slice(EARLY, T)
        scalar_part, vector_part = slice(T - SPLIT, T), slice(0, T - SPLIT)
        kept_2 = gather(2, early, 14)
        kept_3 = gather(3, whole, 12)
        moved_2 = buffer("moved_2", T)
        nc.vector.tensor_tensor(moved_2[:, early], kept_2[:], fresh_high[:, 0, early], ADD)
        moved_1b = add(nc.vector, kept_1b[:], fresh_b[:, 1, :], "moved_1b")
        scatter(1, second, moved_1b[:])
        store(1)
        kept_late = gather(2, late, 14)
        nc.gpsimd.tensor_tensor(moved_2[:, late], kept_late[:], fresh_high[:, 0, late], ADD)
        moved_3 = add(nc.vector, kept_3[:], fresh_high[:, 1, :], "moved_3")
        nc.vector.tensor_copy(listed(windows[2], vector_part), moved_2[:, vector_part])
        scatter(2, scalar_part, moved_2[:, scalar_part])
        nc.vector.tensor_copy(listed(windows[3], whole), moved_3[:])
        store(2)
        store(3)

        sides = [slice(0, SIDE), slice(SIDE, U)]
        pieces = [(slice(0, 384), slice(384, SIDE)), (slice(0, 768 - SIDE), slice(768 - SIDE, U - SIDE))]
        both = turns.tile([P, 2, U, 2], BF16, name="pairs", offset=32 * HALF * 4, align_bytes=64)
        for t in range(2):
            nc.gpsimd.tensor_scalar(both[:, 0, :, t], windows[t][:], 1.0, -0.0, MULT, ADD)
        pairs = [both[:, :, side, :] for side in sides]

        spans = [slice(0, 384), slice(384, 768), slice(768, U)]
        grouped = [
            keep.tile([P, span.stop - span.start, PACK], BF16, name="grouped%d" % c, align_bytes=64)
            for c, span in enumerate(spans)
        ]
        targets = [
            (grouped[0][:], grouped[1][:, : SIDE - 384, :]),
            (grouped[1][:, SIDE - 384 :, :], grouped[2][:]),
        ]
        for e, (copy, word) in enumerate(((nc.vector.tensor_copy, I32), (nc.scalar.copy, U32))):
            copy(out=pairs[e][:, 1, :, 1], in_=windows[3][:, sides[e]])
            for piece in pieces[e]:
                copy(out=pairs[e][:, 1, piece, 0], in_=windows[2][:, sides[e]][:, piece])
            src = pairs[e].rearrange("p h c e -> p h (c e)").bitcast(word).rearrange("p h c -> p c h")
            for piece, target in zip(pieces[e], targets[e]):
                dst = target.rearrange("p c t -> p (c t)").bitcast(word).rearrange("p (c h) -> p c h", h=2)
                copy(out=dst, in_=src[:, piece, :])

        y_plane = keep.tile([P, U], U8, name="y_plane", align_bytes=64)
        y_codes = keep.tile([P, U], I32, name="y_codes", align_bytes=64)
        words_out = out_1[0].rearrange("p n t -> p (n t)").bitcast(I32)
        for span, tile in zip(spans, grouped):
            nc.vector.quantize_mx(
                out=y_codes[:, span].bitcast(FP8X4),
                scales=y_plane[:, span],
                in_=tile[:].rearrange("p c t -> p (c t)"),
            )
            nc.sync.dma_start(words_out[:, span], y_codes[:, span])
        for q in range(4):
            queue = nc.sync if q % 2 else nc.scalar
            queue.dma_start(
                out_2[0, 4 * q : 4 * q + 4, :].bitcast(I32), y_plane[32 * q : 32 * q + 4, :].bitcast(I32)
            )
